import numpy as np, ml_dtypes
CORES = [6,15,38,47]
N = 4
import mx_ref
BF = ml_dtypes.bfloat16
def gentries(a):
    return np.ascontiguousarray(a.reshape(8, 16, -1).transpose(0, 2, 1)).reshape(8, -1)
def gtable(e):
    e = np.asarray(e); return np.ascontiguousarray(e.reshape(8, -1, 16).transpose(0, 2, 1)).reshape(128, -1).astype(np.int32)
def gcols(t, e):
    v = np.concatenate([t.reshape(8, 16, -1, 4), np.zeros((8, 16, 1, 4), BF)], axis=2)
    return np.ascontiguousarray(np.stack([v[g][:, e[g]] for g in range(8)])).reshape(128, -1)
def tile(rs):
    return np.stack(rs, axis=2).reshape(128, -1).astype(BF)
def pick(q, e):
    c = np.concatenate([q[0].reshape(128, -1, 4), np.zeros((128, 1, 4), np.uint8)], axis=1); s = np.concatenate([q[1], np.ones((16, 1), np.uint8)], axis=1)
    return (np.ascontiguousarray(c[:, e].reshape(128, -1)), np.ascontiguousarray(s[:, e]))
def join(*qs):
    return (np.concatenate([q[0] for q in qs], axis=1), np.concatenate([q[1] for q in qs], axis=1))
def put(q, e, v):
    c, s = q[0].reshape(128, -1, 4).copy(), q[1].copy(); c[:, e] = v[0].reshape(128, -1, 4); s[:, e] = v[1]
    return (c.reshape(128, -1), s)
def pk(c, s):
    return (np.ascontiguousarray(c), mx_ref.live(s))
def emit(q):
    return q[0], q[1]
def packed(v, rng):
    q = [mx_ref.quantize(np.ascontiguousarray(v[r])) for r in range(N)]
    return np.stack([a for a, b in q]), np.stack([mx_ref.plane(b, rng) for a, b in q])
def values_of_codes():
    e, c = np.zeros((128, 128, 4), np.float32), np.zeros((128, 2, 4), np.uint8)
    e[np.arange(128), np.arange(128), 0] = 1
    c[:127, :, 0] = np.arange(256).reshape(2, 128).T[:127]
    return mx_ref.matmul(mx_ref.quantize(e.reshape(128, 512).astype(BF)), (c.reshape(128, 8), np.full((16, 2), 127, np.uint8))).T.reshape(-1).astype(np.float64)
CODE_VALUE, SCALE_VALUE = values_of_codes(), 2.0 ** (np.arange(256) - 127.0)
def decode(q):
    return (CODE_VALUE[q[0]].reshape(16, 8, -1, 4) * SCALE_VALUE[q[1]][:, None, :, None] + 0.0).reshape(128, -1).astype(np.float32)
def f(rng, *shape):
    return mx_ref.flush((rng.standard_normal(shape, dtype=np.float32) * np.exp2(rng.integers(-2, 3, shape[:-1] + (1,)))).astype(BF))
def wide(rng, *shape, cols=0):
    v = rng.standard_normal(shape, dtype=np.float32) * np.exp2(rng.integers(-12, 13, shape)).astype(np.float32)
    if cols: v *= np.repeat(np.exp2(rng.integers(-cols, cols + 1, shape[:-2] + (1, shape[-1] // 4))) * (rng.random(shape[:-2] + (1, shape[-1] // 4)) > 0.0625), 4, axis=-1).astype(np.float32)
    return mx_ref.flush(v.astype(BF))
C, H = 448, 224
STEP = [1, 2, 3]
def numbers_of(rng):
    return {"x": np.array(f(rng, N, 128, 4 * C)), "u": np.array(f(rng, N, 128, 512)), "v": np.array(f(rng, N, 128, 512))}
def stored(k):
    return {"nl": np.stack([gtable(k[r]) for r in range(N)])}
def lists(rng):
    return stored(rng.permuted(np.tile(np.arange(C), (N, 8, 1)), axis=2))
def layers(rng, still=()):
    w = np.array(f(rng, N, 128, 2048)).reshape(N, 8, 16, 4, 8, 16, 4)
    for i in still:
        w[:, :, i] = 0
        w[:, :, :, :, :, i] = 0
    return w
def weights(rng, w):
    c, p = packed(np.ascontiguousarray(w).reshape(N, 128, 2048), rng)
    return {"wc": c, "ws": p}
def setup_inputs(rng):
    return {**numbers_of(rng), **lists(rng), **weights(rng, layers(rng))}
def setup_inputs_ties(rng):
    d = numbers_of(rng)
    o = rng.permutation(N)
    k = rng.integers(-1, 2, (N, 8, 3, C)).astype(np.float32)
    k[o[1]] = 1
    x = d["x"].reshape(N, 8, 16, C, 4)
    x[:, :, :3] = 0
    x[:, :, :3, :, 0] = k.astype(BF)
    c = np.ones(N, np.float32)
    c[o[0]] = 0
    c[o[2]] = -1
    u = d["u"].reshape(N, 8, 16, 8, 16, 4)
    u[:, :, :, :, :3] = 0
    g = np.arange(8)
    for j in range(3): u[:, g, j, g, j, 0] = c.astype(BF)[:, None]
    w = layers(rng)
    w[:, :, :, :, :, :8] = 0
    return {"x": x.reshape(N, 128, 4 * C), "u": u.reshape(N, 128, 512), "v": d["v"], **lists(rng), **weights(rng, w)}
def setup_inputs_near(rng):
    d = numbers_of(rng)
    o = rng.permutation(N) % 3
    x = d["x"].astype(np.float32).reshape(N, 8, 16, C, 4)
    u = d["u"].astype(np.float32).reshape(N, 8, 16, 8, 16, 4)
    w = layers(rng, range(8))
    x[:, :, :8] = 0
    u[:, :, :, :, :3] = 0
    g = np.arange(8)
    for r in range(N):
        k, e = (1.0, 1.0) if o[r] == 0 else (2.0 ** -28, 2.0 ** -30)
        if o[r] == 2:
            x[r, :, 8:] = 0
            x[r, :, 8, :, 0] = k
            w[r] = 0
        for j in range(3):
            u[r, g, 6, g, j, 0] = e
            if o[r] < 2:
                s = rng.integers(-1, 2, (8, C)) * k
                x[r, :, 2 * j, :, 0] = 1.125 * s
                x[r, :, 2 * j + 1, :, 0] = -1.25 * s
                u[r, g, 2 * j, g, j, 0] = 1.125 * e
                u[r, g, 2 * j + 1, g, j, 0] = e
            else:
                x[r, :, 9 + j, :, 0] = k * rng.choice([-1.0, 1.0], (8, C))
                u[r, g, 12 + j, g, j, 0] = e
                w[r, g, 9 + j, 0, g, 12 + j, 0] = 2.0 ** -8
        at = [0, C - 1, int(rng.integers(C)), int(rng.integers(C))]
        for h, c in zip(rng.permutation(8)[:4], at): x[r, h, 6, c, 0] = 2.0 ** 30 * rng.choice([-1.0, 1.0])
    return {"x": x.reshape(N, 128, 4 * C).astype(BF), "u": u.reshape(N, 128, 512).astype(BF), "v": d["v"], **lists(rng), **weights(rng, w)}
def setup_inputs_odd(rng):
    d = numbers_of(rng)
    x = (1.0 + (2 * rng.integers(0, 64, (N, 16, 8, C, 4)) + 1) * 2.0 ** -7) * np.exp2(-rng.integers(0, 7, (N, 16, 8, C, 4)).astype(np.float64)) * rng.choice([-1.0, 1.0], (N, 16, 8, C, 4))
    x[:, :, 0, :, 0] = 1.96875 * 2.0 ** 8 * rng.choice([-1.0, 1.0], (N, 16, 1))
    u = d["u"].reshape(N, 16, 8, 128, 4)
    u[:, :, 0] = 0
    return {"x": x.astype(np.float32).reshape(N, 128, 4 * C).astype(BF), "u": u.reshape(N, 128, 512), "v": d["v"], **lists(rng), **weights(rng, layers(rng, (0, 8)))}
def setup_inputs_ends(rng):
    d = numbers_of(rng)
    o, e = rng.permutation(N) % 4, rng.permutation(N) % 4
    x = np.zeros((N, 8, 16, C, 4))
    u = d["u"].astype(np.float32).reshape(N, 8, 16, 8, 16, 4)
    v = d["v"].astype(np.float32)
    w = np.zeros((N, 8, 16, 4, 8, 16, 4), np.float32)
    k = np.tile(np.arange(C), (N, 8, 1))
    def sized(small, low, *q):
        return (1.0 + 0.125 * rng.integers(0, 8, q)) * 2.0 ** -30 if small else (low + 0.1 * rng.random(q)) * 2.0 ** 30
    for r in range(N):
        h = rng.permutation(8)
        c = np.where(h < 2, 0.0, h % 2 * 2.0 - 1.0)[:, None] * np.where((h > 5)[:, None], [1.0, -1.0, 1.0], 1.0)
        c = c[None, None, :, :, None]
        if o[r] == 3:
            x[r] = d["x"][r].astype(np.float32).reshape(8, 16, C, 4)[:, :, :1]
            u[r, :, :, :, :3] *= np.abs(c).astype(np.float32)
        else:
            small = o[r] == 2
            x[r] = sized(small, 0.7, 8, 16, C, 4) * (rng.choice([-1.0, 1.0], (C, 1)) if o[r] == 1 else -1.0)
            u[r, :, :, :, :3] = c * sized(small, 0.9, 8, 16, 8, 3, 4)
            v[r] = sized(small, 0.9, 128, 512) * rng.choice([-1.0, 1.0], (128, 512))
        if o[r] != 2: x[r, :, 14:] = 0
        i, last = np.arange(14), np.arange(14, 16)
        for g in range(8):
            for b in range(4):
                w[r, g, i, b, g, i, b] = 2.0 ** -8 if o[r] == 3 else 2.0
                if o[r] == 2: w[r, g, last, b, g, last, b] = 256.0
        if e[r] == 1: k[r] = C - 1 - np.arange(C)
        if e[r] == 2:
            k[r, :, :H] = 2 * np.arange(H)
            k[r, :, H:] = 2 * np.arange(H)[::-1] + 1
        if e[r] == 3: k[r] = rng.permuted(k[r], axis=1)
    return {"x": x.astype(np.float32).reshape(N, 128, 4 * C).astype(BF), "u": u.reshape(N, 128, 512).astype(BF), "v": v.astype(BF), **stored(k), **weights(rng, w.astype(BF))}
def setup_inputs_spread(rng):
    d = setup_inputs(rng)
    d["x"] = wide(rng, N, 128, 4 * C, cols=6)
    return d
def check_inputs(d):
    b = []
    for k in ("x", "u", "v"):
        a = np.abs(d[k].astype(np.float32))
        if not (np.isfinite(a).all() and ((a == 0) | (a >= 2.0 ** -30) & (a <= 2.0 ** 30)).all()): b.append("a value of " + k)
    none, least, most = [emit(mx_ref.quantize(np.full((128, 16), k, np.float32).astype(BF)))[1][0, 0] for k in (0.0, 2.0 ** -8, 2.0 ** 8)]
    for r in range(N):
        if (np.sort(gentries(d["nl"][r]), axis=1) != np.arange(C)).any(): b.append("nl: a list that is no permutation")
        if ((d["wc"][r] == 0x7F) | (d["wc"][r] == 0xFF)).any(): b.append("wc: a code that is no number")
        s = mx_ref.live(d["ws"][r])
        if ((s != none) & ((s < least) | (s > most))).any(): b.append("ws: a scale out of range")
        if (((d["wc"][r].reshape(16, 8, 512, 4) & 0x7F) != 0) & (s == none)[:, None, :, None]).any(): b.append("wc: a code other than zero under the scale of zeros")
    return b
def ends(n):
    return np.take_along_axis(np.argsort(n, axis=1), n ^ 1, axis=1)
def reference(x, u, v, nl, wc, ws):
    qu = [mx_ref.quantize(u[r]) for r in range(N)]
    lay = [pk(wc[r], ws[r]) for r in range(N)]
    name = [gentries(nl[r]).astype(np.int64) for r in range(N)]
    now = [x[r] for r in range(N)]
    for step in STEP:
        z = []
        for r in range(N):
            s = mx_ref.matmul(qu[r], mx_ref.quantize(now[r])).reshape(8, 16, C)
            for j in range(3):
                d = ends(name[r])
                h = np.where(name[r] % 2 == 0, np.arange(C), d)
                flag = np.take_along_axis(s[:, j], h, axis=1) > 0
                then = np.roll(name[r], -1, axis=0)
                name[r] = np.roll(np.where(flag, np.take_along_axis(then, d, axis=1), then), 1, axis=0)
            z.append(((gcols(now[r], name[r]).astype(np.float32) + gcols(now[r], ends(name[r])).astype(np.float32)) * np.float32(0.5)).astype(BF))
        made = []
        for r in range(N):
            p = (r - step) % N
            m = np.take_along_axis(np.argsort(name[p], axis=1), name[r], axis=1)
            far = gcols(decode(mx_ref.quantize(z[p])).astype(BF), m[:, :H])
            q = mx_ref.quantize(np.ascontiguousarray(np.concatenate([far, gcols(z[r], m[:, H:])], axis=1)))
            made.append(tile([now[r][:, b::4].astype(np.float32) + mx_ref.matmul(pick(lay[r], np.arange(128 * b, 128 * b + 128)), q) * np.float32(0.03125) for b in range(4)]))
        now = made
    y, nm = np.zeros((N, 128, C), np.float32), np.zeros((N, 8, C), np.float32)
    oc, osc = np.zeros((N, 128, 4 * C), np.uint8), np.zeros((N, 16, C), np.uint8)
    for r in range(N):
        q = mx_ref.quantize(now[r])
        y[r] = mx_ref.matmul(mx_ref.quantize(v[r]), q)
        nm[r] = name[r]
        oc[r], osc[r] = emit(q)
    return {"y": y, "nm": nm, "oc": oc, "osc": osc}

@@ -1,0 +1,517 @@
+from concourse.bass import DstId, RemoteDMATransfer
+from concourse.mybir import dt, AluOpType, ActivationFunctionType
+import comms_topo
+
+C, H = 448, 224
+STEP = [1, 2, 3]
+K, BIG = 512.0, 2048.0
+NROW, NLIST = 40, 48
+
+SCRATCH = {
+    "xt": ("sbuf", [128, 4 * C], "bfloat16"),
+    "xh": ("sbuf", [128, 2 * 4 * C], "bfloat16"),
+    "xb": ("sbuf", [128, 4 * C], "bfloat16"),
+    "tmp": ("sbuf", [128, 4 * C], "float32"),
+    "za": ("sbuf", [128, 2 * 4 * H], "bfloat16"),
+    "zt": ("sbuf", [128, 4 * H], "bfloat16"),
+    "vt": ("sbuf", [128, 4 * C], "bfloat16"),
+    "ut": ("sbuf", [128, 512], "bfloat16"),
+    "vi": ("sbuf", [128, 512], "bfloat16"),
+    "one": ("sbuf", [128, 512], "bfloat16"),
+    "et": ("sbuf", [128, 4 * 512], "bfloat16"),
+    "yo": ("sbuf", [128, C], "float32"),
+    "wq": ("sbuf", [128, 512], "float8_e4m3fn_x4"), "wp": ("sbuf", [128, 512], "uint8"),
+    "uq": ("sbuf", [128, 128], "float8_e4m3fn_x4"), "us": ("sbuf", [128, 128], "uint8"),
+    "pq": ("sbuf", [128, 384], "float8_e4m3fn_x4"), "ps": ("sbuf", [128, 384], "uint8"),
+    "vq": ("sbuf", [128, 128], "float8_e4m3fn_x4"), "vs": ("sbuf", [128, 128], "uint8"),
+    "eq": ("sbuf", [128, 512], "float8_e4m3fn_x4"), "es": ("sbuf", [128, 512], "uint8"),
+    "xq": ("sbuf", [128, C], "float8_e4m3fn_x4"), "xs": ("sbuf", [128, C], "uint8"),
+    "zq": ("sbuf", [128, 3 * H], "float8_e4m3fn_x4"), "zs": ("sbuf", [128, 3 * H], "uint8"),
+    "lq": ("sbuf", [128, 3 * H], "float8_e4m3fn_x4"), "ls": ("sbuf", [128, 3 * H], "uint8"),
+    "mq": ("sbuf", [128, C], "float8_e4m3fn_x4"), "ms": ("sbuf", [128, C], "uint8"),
+    "rows": ("sbuf", [128, NROW * C], "float32"),
+    "lf": ("sbuf", [128, NLIST * 32], "float32"),
+    "lu": ("sbuf", [128, NLIST * 32], "uint16"),
+    "li": ("sbuf", [128, NLIST * 32], "int32"),
+    "fl": ("sbuf", [128, 3 * C], "bfloat16"),
+    "fr": ("sbuf", [128, 4 * C], "bfloat16"),
+    "nl2": ("sbuf", [128, 56], "int32"), "nb2": ("sbuf", [128, 56], "int32"),
+    "nw2": ("sbuf", [128, 56], "int32"), "nx2": ("sbuf", [128, 56], "int32"),
+    "nu2": ("sbuf", [128, 56], "uint16"), "nxu2": ("sbuf", [128, 56], "uint16"),
+    "own": ("sbuf", [128, 64], "float32"), "shf": ("sbuf", [128, 64], "float32"),
+    "sg": ("sbuf", [128, 128], "float32"),
+    "req": ("sbuf", [128, 3 * 32], "uint16"), "inv": ("sbuf", [128, 3 * 32], "uint16"),
+    "lreq": ("sbuf", [128, 3 * 32], "uint16"), "linv": ("sbuf", [128, 3 * 32], "uint16"),
+    "iot": ("sbuf", [128, C], "float32"), "hf": ("sbuf", [128, 2 * C], "float32"), "hb": ("sbuf", [128, C], "bfloat16"),
+    "ri": ("sbuf", [128, 2 * C], "int32"), "pc": ("sbuf", [128, 8], "int32"), "pf": ("sbuf", [128, 8], "float32"),
+    "ci": ("sbuf", [128, 32], "int32"), "cl": ("sbuf", [128, 64], "float32"),
+    "pk": ("sbuf", [128, 48], "int32"), "pu": ("sbuf", [128, 48], "uint16"),
+    "pb": ("psum", [128, 4096], "float32"),
+}
+SEMAPHORES = ["sv", "ss", "st", "sg"] + ["d%d" % k for k in range(64)] + ["%s%d" % (n, k) for n in ("rr", "ri", "rc", "kr", "ki", "kc") for k in range(3)]
+CODES = ("wq", "uq", "pq", "vq", "eq", "xq", "zq", "lq", "mq")
+
+
+def overlap(a, b):
+    if a[0] != b[0] or a[2] <= b[1] or b[2] <= a[1] or a[4] <= b[3] or b[4] <= a[3]:
+        return False
+    if a[5] == b[5] and a[5] > 1:
+        return (a[3] - b[3]) % a[5] == 0
+    return True
+
+
+def covers(a, b):
+    if a[1] > b[1] or a[2] < b[2] or a[3] > b[3] or a[4] < b[4]:
+        return False
+    return a[5] == 1 or (a[5] == b[5] and (a[3] - b[3]) % a[5] == 0)
+
+
+def rank_program(g, core, T, topo):
+    rank = T.rank_of(core)
+    if rank is None:
+        return
+    Op, Act = AluOpType, ActivationFunctionType
+    queue = {"V": g.vector, "S": g.scalar, "P": g.tensor, "G": g, "Y": g.sync}
+    esem = {"V": "sv", "S": "ss", "P": "st", "G": "sg"}
+    total, clock, log, nd = {}, {q: {} for q in queue}, {}, [0]
+
+    def region(name, c0, c1, step=1, p0=0, p1=128):
+        if name == "pb":
+            return (name, 0, 128, c0 // 512 * 512, (c1 + 511) // 512 * 512, 1)
+        return (name, p0, p1, c0, c1, step)
+
+    def A(name, c0, c1, step=1, p0=0, p1=128, pstep=1, bits=None):
+        t = T[name]
+        rows = slice(None) if (p0, p1, pstep) == (0, 128, 1) else slice(p0, p1, pstep) if pstep > 1 else slice(p0, p1)
+        ap = t[rows, c0:c1] if step == 1 else t[rows, c0:c1:step]
+        if bits is not None: ap = ap.bitcast(bits)
+        return (ap, [region(name, c0, c1, step, p0, p1)])
+
+    def ind(win, off):
+        return (win[0].indirect(off[0]), win[1] + off[1])
+
+    def deps_of(q, ins, outs, dma):
+        deps = []
+        for reg in ins:
+            for kind, r, op in log.get(reg[0], []):
+                if overlap(reg, r):
+                    if kind == "w": deps.append(op)
+                    elif reg[0] == "pb" and op["q"] != q: deps.append(op)
+        for reg in outs:
+            for kind, r, op in log.get(reg[0], []):
+                if overlap(reg, r):
+                    if kind == "r" and op["q"] == q and not op["dma"] and not dma: continue
+                    deps.append(op)
+        return deps
+
+    def waits(q, deps):
+        ck = clock[q]
+        for op in sorted(deps, key=lambda o: -o["n"]):
+            if ck.get(op["sem"], 0) < op["val"]:
+                queue[q].wait_ge(T.sem[op["sem"]], op["val"])
+                for s, v in op["clock"].items(): ck[s] = max(ck.get(s, 0), v)
+                ck[op["sem"]] = max(ck.get(op["sem"], 0), op["val"])
+
+    count = [0]
+
+    def record(op, ins, outs):
+        count[0] += 1
+        op["n"] = count[0]
+        for reg in outs:
+            log[reg[0]] = [e for e in log.get(reg[0], []) if not covers(reg, e[1])] + [("w", reg, op)]
+        for reg in ins:
+            log.setdefault(reg[0], []).append(("r", reg, op))
+
+    def emit(q, fn, outs, ins, dma=False):
+        ri = [r for x in ins for r in x[1]]
+        ro = [r for x in outs for r in x[1]]
+        waits(q, deps_of(q, ri, ro, dma))
+        inst = fn(queue[q])
+        if dma:
+            sem = "d%d" % nd[0]
+            nd[0] += 1
+            n = 16
+        else:
+            sem, n = esem[q], 1
+        inst.then_inc(T.sem[sem], n)
+        total[sem] = total.get(sem, 0) + n
+        op = {"q": q, "dma": dma, "sem": sem, "val": total[sem], "clock": dict(clock[q])}
+        record(op, ri, ro)
+
+    def dma(q, out, in_):
+        emit(q, lambda e: e.dma_start(out[0], in_[0]), [out], [in_], True)
+
+    def src(name, c0=None, c1=None, p0=None, p1=None):
+        t = T[name]
+        return (t[slice(p0, p1), slice(c0, c1)], [])
+
+    def copy(q, out, in_, scale=None):
+        if q == "V":
+            if scale is None: emit("V", lambda e: e.tensor_copy(out[0], in_[0]), [out], [in_])
+            else: emit("V", lambda e: e.tensor_scalar(out[0], in_[0], scale, None, Op.mult), [out], [in_])
+        elif scale is None: emit("S", lambda e: e.activation(out[0], in_[0], Act.Copy), [out], [in_])
+        else: emit("S", lambda e: e.activation(out[0], in_[0], Act.Copy, scale=scale), [out], [in_])
+
+    def tt(out, a, b, op):
+        emit("V", lambda e: e.tensor_tensor(out[0], a[0], b[0], op), [out], [a, b])
+
+    def ts(out, a, s1, op0, s2=None, op1=None):
+        ins = [a] + [s for s in (s1, s2) if isinstance(s, tuple)]
+        v1 = s1[0] if isinstance(s1, tuple) else s1
+        v2 = s2[0] if isinstance(s2, tuple) else s2
+        if op1 is None: emit("V", lambda e: e.tensor_scalar(out[0], a[0], v1, None, op0), [out], ins)
+        else: emit("V", lambda e: e.tensor_scalar(out[0], a[0], v1, v2, op0, op1), [out], ins)
+
+    def quant(qn, sn, a, b, tile):
+        o, s = A(qn, a, b), A(sn, a, b)
+        emit("V", lambda e: e.quantize_mx(o[0], s[0], tile[0]), [o, s], [tile])
+
+    def mm(bank, sq, sp, a, mq, mp, b0, b1):
+        out, l, ls, r, rs = A("pb", 512 * bank, 512 * bank + b1 - b0), A(sq, a, a + 128), A(sp, a, a + 128), A(mq, b0, b1), A(mp, b0, b1)
+        emit("P", lambda e: e.matmul_mx(out[0], l[0], ls[0], r[0], rs[0], True, True), [out], [l, ls, r, rs])
+
+    def bank(k, n=H):
+        return A("pb", 512 * k, 512 * k + n)
+
+    pool = {"rows": [0], "lf": [0], "lu": [0], "li": [0], "fr": [0]}
+    size = {"rows": NROW, "lf": NLIST, "lu": NLIST, "li": NLIST, "fr": 4}
+
+    def new(kind):
+        k = pool[kind][0] % size[kind]
+        pool[kind][0] += 1
+        return (kind, k * (C if kind in ("rows", "fr") else 32))
+
+    def at(slot, a, b, step=1):
+        return A(slot[0], slot[1] + a, slot[1] + b, step)
+
+    IOT = ("iot", 0)
+    kc, thr = A("pf", 0, 1), A("pf", 1, 2)
+    cl, ck = A("cl", 0, 28), A("cl", 32, 60)
+
+    def gather(q, out, win, lu, a=0, b=C, w=C):
+        copy(q, at(out, a, b), ind(at(win, 0, w), at(lu, a // 16, b // 16)))
+
+    def both(out, win, lu, a=0, b=C):
+        h = (b - a) // 64 * 32
+        gather("S", out, win, lu, a + h, b)
+        gather("V", out, win, lu, a, a + h)
+
+    def scan(row, a=0, b=C):
+        o = new("rows")
+        hf, r, out = A("hf", 0, b - a), at(row, a, b), at(o, a, b)
+        emit("V", lambda e: e.tensor_tensor_scan(out[0], hf[0], r[0], 0.0, Op.add, Op.max), [out], [hf, r])
+        return A("rows", o[1] + a + 15, o[1] + b, 16)
+
+    def flags(row):
+        o = new("fr")
+        hb, r, out = A("hb", 0, C), at(row, 0, C), at(o, 0, C)
+        emit("V", lambda e: e.tensor_tensor_scan(out[0], hb[0], r[0], 0.0, Op.add, Op.max), [out], [hb, r])
+        f = new("lf")
+        ts(at(f, 0, 28), A("fr", o[1] + 15, o[1] + C, 16), thr, Op.is_gt)
+        return f
+
+    def remote(dst, out, in_, rsem, lsem):
+        rid, pid, _ = topo.addr(dst)
+        waits("G", deps_of("G", in_[1], [], True))
+        n = len(topo.engines(core, dst))
+        g.remote_dma(out[0], in_[0], T.sem[rsem], T.sem[lsem], pid, rid, topo.mask(core, dst))
+        total[lsem] = total.get(lsem, 0) + n
+        record({"q": "G", "dma": True, "sem": lsem, "val": total[lsem], "clock": dict(clock["G"])}, in_[1], [])
+
+    def arrive(outs, sem, n):
+        total[sem] = n
+        record({"q": "R", "dma": True, "sem": sem, "val": n, "clock": {}}, [], [r for o in outs for r in o[1]])
+
+    dma("Y", A("nl2", 28, 56, p0=16), src("nl", p0=0, p1=112))
+    dma("S", A("nl2", 28, 56, p0=0, p1=16), src("nl", p0=112, p1=128))
+    dma("Y", A("nl2", 0, 28), src("nl"))
+    dma("S", A("xt", 0, 4 * H), src("x", 0, 4 * H))
+    dma("Y", A("ut", 0, 512), src("u"))
+    dma("S", A("xt", 4 * H, 4 * C), src("x", 4 * H, 4 * C))
+    dma("Y", A("wq", 0, 512, bits=dt.uint8), src("wc"))
+    dma("Y", A("wp", 0, 512), src("ws"))
+    dma("Y", A("vi", 0, 512), src("v"))
+
+    def iota(out, pattern, base, cm, f=False):
+        if f: emit("G", lambda e: e.iota(out[0], pattern, base, cm, allow_small_or_imprecise_dtypes=True), [out], [])
+        else: emit("G", lambda e: e.iota(out[0], pattern, base, cm), [out], [])
+    iota(A("pc", 0, 1), [[1, 1]], 0, 1)
+    iota(A("ci", 0, 28), [[16, 28]], 0, 0)
+    iota(A("pk", 0, 8), [[16, 8]], 112, 0)
+    iota(A("pk", 16, 24), [[16, 8]], 1, 0)
+    iota(A("pk", 32, 40), [[16, 8]], 2, 0)
+    iota(A("iot", 0, C), [[1, C]], 0, 0, True)
+    iota(A("ri", 0, C), [[1, C]], 128, -1)
+    one = A("one", 0, 512)
+    emit("V", lambda e: e.memset(one[0], 1.0), [one], [])
+    for b in range(4):
+        et = A("et", 512 * b, 512 * b + 512)
+        emit("G", lambda e: e.affine_select(et[0], one[0], [[1, 512]], Op.is_equal, 0.0, -b, -4), [et], [one])
+    sgall = A("sg", 0, 128)
+    emit("V", lambda e: e.memset(sgall[0], 0.0), [sgall], [])
+    p15 = A("pc", 1, 2)
+    ts(p15, A("pc", 0, 1), 15, Op.bitwise_and)
+    ts(kc, p15, 15.0, Op.is_lt, K, Op.mult)
+    ts(A("pf", 2, 3), p15, 15.0, Op.is_lt, 2.0, Op.mult)
+    ts(thr, A("pf", 2, 3), 0.5, Op.add)
+    copy("V", A("pf", 3, 4), p15)
+    ts(cl, A("ci", 0, 28), A("pf", 3, 4), Op.add)
+    ts(ck, cl, kc, Op.add)
+    ts(A("pk", 8, 16), A("pk", 0, 8), 127, Op.bitwise_and)
+    copy("V", A("pu", 0, 8), A("pk", 8, 16))
+    copy("V", A("pu", 16, 24), A("pk", 16, 24))
+    copy("V", A("pu", 32, 40), A("pk", 32, 40))
+
+    copy("V", A("nu2", 0, 56), A("nl2", 0, 56))
+    ts(A("nb2", 0, 56), A("nl2", 0, 56), 1, Op.bitwise_and)
+    ts(A("nw2", 0, 56), A("nb2", 0, 56), -2.0, Op.mult, 1.0, Op.add)
+    tt(A("nx2", 0, 56), A("nl2", 0, 56), A("nw2", 0, 56), Op.add)
+    copy("V", A("nxu2", 0, 56), A("nx2", 0, 56))
+    r15 = A("ri", C, 2 * C)
+    iot = A("iot", 0, C)
+    ixs = new("rows")
+    scat = ind(at(ixs, 0, C), A("nxu2", 28, 56))
+    emit("V", lambda e: e.tensor_copy(scat[0], iot[0]), [at(ixs, 0, C)], [iot, A("nxu2", 28, 56)])
+    ix0 = new("rows")
+    scat0 = ind(at(ix0, 0, C), A("nxu2", 0, 28))
+    emit("V", lambda e: e.tensor_copy(scat0[0], iot[0]), [at(ix0, 0, C)], [iot, A("nxu2", 0, 28)])
+    drs = new("rows")
+    gather("S", drs, ixs, ("nu2", 28))
+    ts(r15, A("ri", 0, C), 15, Op.bitwise_and)
+    ts(A("hf", 0, C), r15, 0.0, Op.is_equal, -BIG, Op.mult)
+    ts(A("hf", C, 2 * C), r15, 1.0, Op.is_equal, K, Op.mult)
+    tt(A("hf", 0, C), A("hf", 0, C), A("hf", C, 2 * C), Op.add)
+    ts(A("hb", 0, C), A("hf", 0, C), 1.0 / 256, Op.mult)
+    nrow, drow = new("rows"), new("rows")
+    gather("S", drow, ix0, ("nu2", 0))
+    gather("S", nrow, IOT, ("nu2", 0))
+    odd = new("lf")
+    copy("V", at(odd, 0, 28), A("nb2", 28, 56))
+
+    def even_ends(v, odd, out):
+        t, h = new("lf"), new("lf")
+        tt(out, v, ck, Op.subtract)
+        tt(at(t, 0, 28), at(odd, 0, 28), out, Op.mult)
+        return t, h
+    v = scan(drs)
+    dd = new("lf")
+    t, h = even_ends(v, odd, at(dd, 0, 28))
+    tt(at(h, 0, 28), at(t, 0, 28), cl, Op.add)
+    hu = new("lu")
+    copy("V", at(hu, 0, 28), at(h, 0, 28))
+
+    quant("uq", "us", 0, 128, A("ut", 0, 512))
+    for k in range(3):
+        off = A("pu", 16 * k, 16 * k + 8)
+        o = A("pq", 128 * k, 128 * k + 128, bits=dt.uint32)
+        w = ind(A("uq", 0, 128, bits=dt.uint32), off)
+        emit("V", lambda e: e.tensor_copy(o[0], w[0]), [o], [w])
+        o2, w2 = A("ps", 128 * k, 128 * k + 128), ind(A("us", 0, 128), off)
+        emit("V", lambda e: e.tensor_copy(o2[0], w2[0]), [o2], [w2])
+
+    half = [(0, H), (H, C)]
+
+    def states(k):
+        a, b = half[k]
+        quant("xq", "xs", a, b, A("xt", 4 * a, 4 * b))
+
+    def scores(k):
+        a, b = half[k]
+        banks = [3, 4, 5] if k == 0 else [0, 1, 2]
+        for j in range(3):
+            mm(banks[j], "pq", "ps", 128 * j, "xq", "xs", a, b)
+        for j in range(3):
+            o, i = A("fl", C * j + a, C * j + b), bank(banks[j])
+            if j == 0: ts(o, i, 0.0, Op.is_gt)
+            else: emit("S", lambda e: e.activation(o[0], i[0], Act.Sign), [o], [i])
+
+    def planes(rd, k):
+        a, b = half[k]
+        for e in range(4):
+            x = A("xt", 4 * a + e, 4 * b, 4)
+            copy("S", A("xh", 4 * C * (rd % 2) + C * e + a, 4 * C * (rd % 2) + C * e + b), x, 0.5)
+
+    def planes32(k):
+        a, b = half[k]
+        for e in range(4):
+            copy("S", A("xb", C * e + a, C * e + b), A("xt", 4 * a + e, 4 * b, 4), 32.0)
+
+    def shift(sig):
+        t1, t2, t3 = ("sg", 32), ("sg", 64), ("sg", 96)
+        i, o = A("sg", 0, 32), A("sg", 32, 64)
+        emit("V", lambda e: e.transpose(o[0], i[0]), [o], [i])
+        copy("V", A("sg", 80, 96), A("sg", 32, 48))
+        for a in range(4):
+            d = 32 * ((a + 1) % 4)
+            copy("S" if a in (1, 2) else "V", A("sg", 64, 80, p0=d, p1=d + 32), A("sg", 48, 64, p0=32 * a, p1=32 * a + 32))
+        i2, o2 = A("sg", 64, 96), A("sg", 96, 128)
+        emit("V", lambda e: e.transpose(o2[0], i2[0]), [o2], [i2])
+        return A("sg", 96, 124)
+
+    states(1)
+    scores(1)
+    states(0)
+    scores(0)
+    planes(0, 1)
+    for b in range(4):
+        quant("eq", "es", 128 * b, 128 * b + 128, A("et", 512 * b, 512 * b + 512))
+    quant("vq", "vs", 0, 128, A("vi", 0, 512))
+
+    for rd, step in enumerate(STEP):
+        last = rd == 2
+        p, q = T.cores[(rank - step) % 4], T.cores[(rank + step) % 4]
+        for j in range(3):
+            frow = new("fr")
+            both(frow, ("fl", C * j), hu)
+            F = flags(frow)
+            t = new("lf")
+            tt(at(t, 0, 28), at(F, 0, 28), at(dd, 0, 28), Op.mult)
+            su = new("lu")
+            if j == 0:
+                s = new("lf")
+                tt(at(s, 0, 28), at(t, 0, 28), cl, Op.add)
+                copy("V", at(su, 0, 28), at(s, 0, 28))
+            else:
+                tt(A("sg", 0, 28), at(t, 0, 28), cl, Op.add)
+                copy("V", at(su, 0, 28), shift(None))
+            n2 = new("rows")
+            if j == 2:
+                both(n2, nrow, su)
+                nrow = n2
+                break
+            srow, erow, d2 = new("rows"), new("rows"), new("rows")
+            gather("S", srow, IOT, su)
+            gather("V", erow, drow, su)
+            gather("S", n2, nrow, su)
+            v = scan(erow)
+            eu = new("lu")
+            ts(at(eu, 0, 28), v, kc, Op.subtract)
+            both(d2, srow, eu)
+            nv = scan(n2)
+            ni, nb, odd = new("li"), new("li"), new("lf")
+            ts(at(ni, 0, 28), nv, kc, Op.subtract)
+            ts(at(nb, 0, 28), at(ni, 0, 28), 1, Op.bitwise_and)
+            copy("V", at(odd, 0, 28), at(nb, 0, 28))
+            v = scan(d2)
+            dd = new("lf")
+            t, h = even_ends(v, odd, at(dd, 0, 28))
+            tt(at(h, 0, 28), at(t, 0, 28), cl, Op.add)
+            hu = new("lu")
+            copy("V", at(hu, 0, 28), at(h, 0, 28))
+            nrow, drow = n2, d2
+        nu = ("req", 32 * rd)
+        va = scan(nrow, 0, H)
+        ts(at(nu, 0, 14), va, kc, Op.subtract)
+        remote(p, A("lreq", 32 * rd, 32 * rd + 14), at(nu, 0, 14), "rr%d" % rd, "kr%d" % rd)
+        vb = scan(nrow, H, C)
+        ts(at(nu, 14, 28), vb, kc, Op.subtract)
+        ni, nb, nw, nx, nxu = new("li"), new("li"), new("li"), new("li"), new("lu")
+        copy("V", at(ni, 0, 28), at(nu, 0, 28))
+        ts(at(nb, 0, 28), at(ni, 0, 28), 1, Op.bitwise_and)
+        ts(at(nw, 0, 28), at(nb, 0, 28), -2.0, Op.mult, 1.0, Op.add)
+        tt(at(nx, 0, 28), at(ni, 0, 28), at(nw, 0, 28), Op.add)
+        copy("V", at(nxu, 0, 28), at(nx, 0, 28))
+        ix = new("rows")
+        sc = ind(at(ix, 0, C), at(nxu, 0, 28))
+        emit("V", lambda e: e.tensor_copy(sc[0], iot[0]), [at(ix, 0, C)], [iot, at(nxu, 0, 28)])
+        planes(rd, 0)
+        vi = scan(ix)
+        iu = ("inv", 32 * rd)
+        ts(at(iu, 0, 28), vi, kc, Op.subtract)
+        remote(q, A("linv", 32 * rd, 32 * rd + 28), at(iu, 0, 28), "ri%d" % rd, "ki%d" % rd)
+        if last:
+            dma("Y", (T.nm[:, :], []), A("rows", nrow[1], nrow[1] + C, pstep=16))
+        nen = len(topo.engines(core, q))
+        arrive([A("lreq", 32 * rd, 32 * rd + 14)], "rr%d" % rd, nen)
+        nq = ("lreq", 32 * rd)
+        X = [("xh", 4 * C * (rd % 2) + C * e) for e in range(4)]
+        for e in range(4):
+            gather("S", ("za", H * e), X[e], nq, 0, H)
+        brow = new("rows")
+        gather("V", brow, ix, nq, 0, H)
+        bv = scan(brow, 0, H)
+        bu = new("lu")
+        ts(at(bu, 0, 14), bv, kc, Op.subtract)
+        for e in range(4):
+            tt(A("zt", e, 4 * H, 4), ind(at(X[e], 0, C), at(bu, 0, 14)), A("za", H * e, H * e + H), Op.add)
+        zc, zp = A("zq", H * rd, H * rd + H), A("zs", H * rd, H * rd + H)
+        zt = A("zt", 0, 4 * H)
+        emit("V", lambda e: e.quantize_mx(zc[0], zp[0], zt[0]), [zc, zp], [zt])
+        remote(q, A("lq", H * rd, H * rd + H, bits=dt.uint8), A("zq", H * rd, H * rd + H, bits=dt.uint8), "rc%d" % rd, "kc%d" % rd)
+        remote(q, A("ls", H * rd, H * rd + H), zp, "rc%d" % rd, "kc%d" % rd)
+        drow = new("rows")
+        gather("S", drow, ix, nu)
+        arrive([A("linv", 32 * rd, 32 * rd + 28)], "ri%d" % rd, len(topo.engines(core, p)))
+        ip, mrow = new("rows"), new("rows")
+        both(ip, IOT, ("linv", 32 * rd))
+        both(mrow, ip, nxu, H, C)
+        mv = scan(mrow, H, C)
+        mu = new("lu")
+        ts(at(mu, 14, 28), mv, kc, Op.subtract)
+        er, dr = new("rows"), new("rows")
+        gather("S", er, nrow, mu, H, C)
+        gather("V", dr, drow, mu, H, C)
+        ev = scan(er, H, C)
+        eu, du = new("lu"), new("lu")
+        ts(at(eu, 14, 28), ev, kc, Op.subtract)
+        for e in range(4):
+            copy("S", A("za", 4 * H + H * e, 4 * H + H * e + H), ind(at(X[e], 0, C), at(eu, 14, 28)))
+        dv = scan(dr, H, C)
+        ts(at(du, 14, 28), dv, kc, Op.subtract)
+        if rd == 0: planes32(1)
+        for e in range(4):
+            tt(A("vt", 4 * H + e, 4 * C, 4), ind(at(X[e], 0, C), at(du, 14, 28)), A("za", 4 * H + H * e, 4 * H + H * e + H), Op.add)
+        quant("mq", "ms", H, C, A("vt", 4 * H, 4 * C))
+        for e in range(4):
+            mm(e, "wq", "wp", 128 * e, "mq", "ms", H, C)
+        if not last:
+            v = scan(drow)
+            odd = new("lf")
+            copy("V", at(odd, 0, 28), at(nb, 0, 28))
+            t, h = even_ends(v, odd, A("own", 0, 28))
+            tt(A("own", 28, 56), at(t, 0, 28), cl, Op.add)
+            dma("Y", A("shf", 0, 56, p0=16), A("own", 0, 56, p0=0, p1=112))
+            dma("Y", A("shf", 0, 56, p0=0, p1=16), A("own", 0, 56, p0=112, p1=128))
+
+        def new_state(k, banks):
+            a, b = half[k]
+            for e in range(4):
+                o = A("tmp", C * e + a, C * e + b)
+                tt(o, bank(banks[e]), A("xb", C * e + a, C * e + b), Op.add)
+                copy("S", A("xt", 4 * a + e, 4 * b, 4), o, 0.03125)
+            states(k)
+
+        def finish(k):
+            a, b = half[k]
+            bk = 7 if k == 0 else 0
+            mm(bk, "vq", "vs", 0, "xq", "xs", a, b)
+            dma("Y", (T.oc[:, 4 * a:4 * b], []), A("xq", a, b, bits=dt.uint8))
+            for i in range(4):
+                dma("Y" if i % 2 else "S", (T.osc[4 * i:4 * i + 4, a:b], []), A("xs", a, b, p0=32 * i, p1=32 * i + 4))
+            copy("V", A("yo", a, b), bank(bk))
+            dma("Y", (T.y[:, a:b], []), A("yo", a, b))
+
+        planes32(0)
+        new_state(1, [0, 1, 2, 3])
+        if last: finish(1)
+        else:
+            scores(1)
+            planes(rd + 1, 1)
+            planes32(1)
+            dd, hu = ("shf", 0), new("lu")
+            copy("V", at(hu, 0, 28), A("shf", 28, 56))
+        arrive([A("lq", H * rd, H * rd + H), A("ls", H * rd, H * rd + H)], "rc%d" % rd, 2 * len(topo.engines(core, p)))
+        for e in range(4):
+            mm(4 + e, "eq", "es", 128 * e, "lq", "ls", H * rd, H * rd + H)
+        for e in range(4):
+            copy("S" if e % 2 else "V", A("vt", e, 4 * H, 4), bank(4 + e))
+        quant("mq", "ms", 0, H, A("vt", 0, 4 * H))
+        for e in range(4):
+            mm(4 + e, "wq", "wp", 128 * e, "mq", "ms", 0, H)
+        new_state(0, [4, 5, 6, 7])
+        if last: finish(0)
+        else: scores(0)
+
+    for s in sorted(total):
+        if clock["G"].get(s, 0) < total[s]:
+            g.wait_ge(T.sem[s], total[s])

@@ -1,15 +1,13 @@
-from concourse.bass import DstId, RemoteDMATransfer
 from concourse.mybir import dt, AluOpType, ActivationFunctionType
-import comms_topo
 
 C, H = 448, 224
 STEP = [1, 2, 3]
 K, BIG = 512.0, 2048.0
-NROW, NLIST = 40, 48
+NROW, NLIST, NHALF, NSIGN = 32, 48, 16, 10
 
 SCRATCH = {
     "xt": ("sbuf", [128, 4 * C], "bfloat16"),
-    "xh": ("sbuf", [128, 2 * 4 * C], "bfloat16"),
+    "xh": ("sbuf", [128, 4 * C], "bfloat16"),
     "xb": ("sbuf", [128, 4 * C], "bfloat16"),
     "tmp": ("sbuf", [128, 4 * C], "float32"),
     "za": ("sbuf", [128, 2 * 4 * H], "bfloat16"),
@@ -29,27 +27,28 @@ SCRATCH = {
     "zq": ("sbuf", [128, 3 * H], "float8_e4m3fn_x4"), "zs": ("sbuf", [128, 3 * H], "uint8"),
     "lq": ("sbuf", [128, 3 * H], "float8_e4m3fn_x4"), "ls": ("sbuf", [128, 3 * H], "uint8"),
     "mq": ("sbuf", [128, C], "float8_e4m3fn_x4"), "ms": ("sbuf", [128, C], "uint8"),
-    "rows": ("sbuf", [128, NROW * C], "float32"),
+    "rows": ("sbuf", [128, NROW * C], "float32"), "hr": ("sbuf", [128, NHALF * C], "float16"), "fr": ("sbuf", [128, NSIGN * C], "bfloat16"),
     "lf": ("sbuf", [128, NLIST * 32], "float32"),
     "lu": ("sbuf", [128, NLIST * 32], "uint16"),
     "li": ("sbuf", [128, NLIST * 32], "int32"),
     "fl": ("sbuf", [128, 3 * C], "bfloat16"),
-    "fr": ("sbuf", [128, 4 * C], "bfloat16"),
+    "pr": ("sbuf", [128, 3 * C], "bfloat16"),
     "nl2": ("sbuf", [128, 56], "int32"), "nb2": ("sbuf", [128, 56], "int32"),
     "nw2": ("sbuf", [128, 56], "int32"), "nx2": ("sbuf", [128, 56], "int32"),
     "nu2": ("sbuf", [128, 56], "uint16"), "nxu2": ("sbuf", [128, 56], "uint16"),
-    "own": ("sbuf", [128, 64], "float32"), "shf": ("sbuf", [128, 64], "float32"),
+    "own": ("sbuf", [128, 2 * 64], "float32"), "shf": ("sbuf", [128, 2 * 64], "float32"),
     "sg": ("sbuf", [128, 128], "float32"),
     "req": ("sbuf", [128, 3 * 32], "uint16"), "inv": ("sbuf", [128, 3 * 32], "uint16"),
     "lreq": ("sbuf", [128, 3 * 32], "uint16"), "linv": ("sbuf", [128, 3 * 32], "uint16"),
-    "iot": ("sbuf", [128, C], "float32"), "hf": ("sbuf", [128, 2 * C], "float32"), "hb": ("sbuf", [128, C], "bfloat16"),
-    "ri": ("sbuf", [128, 2 * C], "int32"), "pc": ("sbuf", [128, 8], "int32"), "pf": ("sbuf", [128, 8], "float32"),
+    "iot": ("sbuf", [128, C], "float32"), "par": ("sbuf", [128, C], "bfloat16"),
+    "hf": ("sbuf", [128, C], "float32"), "hh": ("sbuf", [128, C], "float16"), "hb": ("sbuf", [128, C], "bfloat16"),
+    "hs": ("sbuf", [128, 96], "float32"), "ri": ("sbuf", [128, 96], "int32"), "tu": ("sbuf", [128, 32], "uint16"),
+    "pc": ("sbuf", [128, 8], "int32"), "pf": ("sbuf", [128, 8], "float32"),
     "ci": ("sbuf", [128, 32], "int32"), "cl": ("sbuf", [128, 64], "float32"),
     "pk": ("sbuf", [128, 48], "int32"), "pu": ("sbuf", [128, 48], "uint16"),
     "pb": ("psum", [128, 4096], "float32"),
 }
 SEMAPHORES = ["sv", "ss", "st", "sg"] + ["d%d" % k for k in range(64)] + ["%s%d" % (n, k) for n in ("rr", "ri", "rc", "kr", "ki", "kc") for k in range(3)]
-CODES = ("wq", "uq", "pq", "vq", "eq", "xq", "zq", "lq", "mq")
 
 
 def overlap(a, b):
@@ -73,7 +72,7 @@ def rank_program(g, core, T, topo):
     Op, Act = AluOpType, ActivationFunctionType
     queue = {"V": g.vector, "S": g.scalar, "P": g.tensor, "G": g, "Y": g.sync}
     esem = {"V": "sv", "S": "ss", "P": "st", "G": "sg"}
-    total, clock, log, nd = {}, {q: {} for q in queue}, {}, [0]
+    total, clock, log, nd, count = {}, {q: {} for q in queue}, {}, [0], [0]
 
     def region(name, c0, c1, step=1, p0=0, p1=128):
         if name == "pb":
@@ -112,8 +111,6 @@ def rank_program(g, core, T, topo):
                 for s, v in op["clock"].items(): ck[s] = max(ck.get(s, 0), v)
                 ck[op["sem"]] = max(ck.get(op["sem"], 0), op["val"])
 
-    count = [0]
-
     def record(op, ins, outs):
         count[0] += 1
         op["n"] = count[0]
@@ -135,15 +132,13 @@ def rank_program(g, core, T, topo):
             sem, n = esem[q], 1
         inst.then_inc(T.sem[sem], n)
         total[sem] = total.get(sem, 0) + n
-        op = {"q": q, "dma": dma, "sem": sem, "val": total[sem], "clock": dict(clock[q])}
-        record(op, ri, ro)
+        record({"q": q, "dma": dma, "sem": sem, "val": total[sem], "clock": dict(clock[q])}, ri, ro)
 
     def dma(q, out, in_):
         emit(q, lambda e: e.dma_start(out[0], in_[0]), [out], [in_], True)
 
     def src(name, c0=None, c1=None, p0=None, p1=None):
-        t = T[name]
-        return (t[slice(p0, p1), slice(c0, c1)], [])
+        return (T[name][slice(p0, p1), slice(c0, c1)], [])
 
     def copy(q, out, in_, scale=None):
         if q == "V":
@@ -151,6 +146,9 @@ def rank_program(g, core, T, topo):
             else: emit("V", lambda e: e.tensor_scalar(out[0], in_[0], scale, None, Op.mult), [out], [in_])
         elif scale is None: emit("S", lambda e: e.activation(out[0], in_[0], Act.Copy), [out], [in_])
         else: emit("S", lambda e: e.activation(out[0], in_[0], Act.Copy, scale=scale), [out], [in_])
+
+    def act(out, in_, func):
+        emit("S", lambda e: e.activation(out[0], in_[0], func), [out], [in_])
 
     def tt(out, a, b, op):
         emit("V", lambda e: e.tensor_tensor(out[0], a[0], b[0], op), [out], [a, b])
@@ -173,42 +171,39 @@ def rank_program(g, core, T, topo):
     def bank(k, n=H):
         return A("pb", 512 * k, 512 * k + n)
 
-    pool = {"rows": [0], "lf": [0], "lu": [0], "li": [0], "fr": [0]}
-    size = {"rows": NROW, "lf": NLIST, "lu": NLIST, "li": NLIST, "fr": 4}
+    pool = {"rows": [0], "lf": [0], "lu": [0], "li": [0], "fr": [0], "hr": [0]}
+    size = {"rows": NROW, "lf": NLIST, "lu": NLIST, "li": NLIST, "fr": NSIGN, "hr": NHALF}
 
     def new(kind):
         k = pool[kind][0] % size[kind]
         pool[kind][0] += 1
-        return (kind, k * (C if kind in ("rows", "fr") else 32))
+        return (kind, k * (C if kind in ("rows", "fr", "hr") else 32))
 
-    def at(slot, a, b, step=1):
+    def at(slot, a=0, b=28, step=1):
         return A(slot[0], slot[1] + a, slot[1] + b, step)
 
     IOT = ("iot", 0)
-    kc, thr = A("pf", 0, 1), A("pf", 1, 2)
+    kc, kb, kc1 = A("pf", 0, 1), A("pf", 1, 2), A("pf", 2, 3)
     cl, ck = A("cl", 0, 28), A("cl", 32, 60)
 
-    def gather(q, out, win, lu, a=0, b=C, w=C):
-        copy(q, at(out, a, b), ind(at(win, 0, w), at(lu, a // 16, b // 16)))
+    def gather(q, out, win, lu, a=0, b=C):
+        copy(q, at(out, a, b), ind(at(win, 0, C), at(lu, a // 16, b // 16)))
 
     def both(out, win, lu, a=0, b=C):
         h = (b - a) // 64 * 32
         gather("S", out, win, lu, a + h, b)
         gather("V", out, win, lu, a, a + h)
 
-    def scan(row, a=0, b=C):
-        o = new("rows")
-        hf, r, out = A("hf", 0, b - a), at(row, a, b), at(o, a, b)
-        emit("V", lambda e: e.tensor_tensor_scan(out[0], hf[0], r[0], 0.0, Op.add, Op.max), [out], [hf, r])
-        return A("rows", o[1] + a + 15, o[1] + b, 16)
+    def scan(row, a=0, b=C, o=None):
+        o = o or new(row[0])
+        hold, r, out = A({"rows": "hf", "hr": "hh", "fr": "hb"}[row[0]], 0, b - a), at(row, a, b), at(o, a, b)
+        emit("V", lambda e: e.tensor_tensor_scan(out[0], hold[0], r[0], 0.0, Op.add, Op.max), [out], [hold, r])
+        return at(o, a + 15, b, 16)
 
-    def flags(row):
-        o = new("fr")
-        hb, r, out = A("hb", 0, C), at(row, 0, C), at(o, 0, C)
-        emit("V", lambda e: e.tensor_tensor_scan(out[0], hb[0], r[0], 0.0, Op.add, Op.max), [out], [hb, r])
-        f = new("lf")
-        ts(at(f, 0, 28), A("fr", o[1] + 15, o[1] + C, 16), thr, Op.is_gt)
-        return f
+    def offsets(v, out=None, a=0, b=28):
+        out = out or new("lu")
+        ts(at(out, a, b), v, kc, Op.subtract)
+        return out
 
     def remote(dst, out, in_, rsem, lsem):
         rid, pid, _ = topo.addr(dst)
@@ -225,9 +220,9 @@ def rank_program(g, core, T, topo):
     dma("Y", A("nl2", 28, 56, p0=16), src("nl", p0=0, p1=112))
     dma("S", A("nl2", 28, 56, p0=0, p1=16), src("nl", p0=112, p1=128))
     dma("Y", A("nl2", 0, 28), src("nl"))
+    dma("S", A("ut", 0, 512), src("u"))
+    dma("Y", A("xt", 4 * H, 4 * C), src("x", 4 * H, 4 * C))
     dma("S", A("xt", 0, 4 * H), src("x", 0, 4 * H))
-    dma("Y", A("ut", 0, 512), src("u"))
-    dma("S", A("xt", 4 * H, 4 * C), src("x", 4 * H, 4 * C))
     dma("Y", A("wq", 0, 512, bits=dt.uint8), src("wc"))
     dma("Y", A("wp", 0, 512), src("ws"))
     dma("Y", A("vi", 0, 512), src("v"))
@@ -235,79 +230,65 @@ def rank_program(g, core, T, topo):
     def iota(out, pattern, base, cm, f=False):
         if f: emit("G", lambda e: e.iota(out[0], pattern, base, cm, allow_small_or_imprecise_dtypes=True), [out], [])
         else: emit("G", lambda e: e.iota(out[0], pattern, base, cm), [out], [])
+
+    def memset(out, k):
+        emit("V", lambda e: e.memset(out[0], k), [out], [])
+
     iota(A("pc", 0, 1), [[1, 1]], 0, 1)
     iota(A("ci", 0, 28), [[16, 28]], 0, 0)
+    iota(A("ri", 0, 16), [[1, 16]], 128, -1)
+    iota(A("ri", 32, 48), [[1, 16]], 0, 0)
+    iota(A("iot", 0, C), [[1, C]], 0, 0, True)
     iota(A("pk", 0, 8), [[16, 8]], 112, 0)
     iota(A("pk", 16, 24), [[16, 8]], 1, 0)
     iota(A("pk", 32, 40), [[16, 8]], 2, 0)
-    iota(A("iot", 0, C), [[1, C]], 0, 0, True)
-    iota(A("ri", 0, C), [[1, C]], 128, -1)
-    one = A("one", 0, 512)
-    emit("V", lambda e: e.memset(one[0], 1.0), [one], [])
-    for b in range(4):
-        et = A("et", 512 * b, 512 * b + 512)
-        emit("G", lambda e: e.affine_select(et[0], one[0], [[1, 512]], Op.is_equal, 0.0, -b, -4), [et], [one])
-    sgall = A("sg", 0, 128)
-    emit("V", lambda e: e.memset(sgall[0], 0.0), [sgall], [])
-    p15 = A("pc", 1, 2)
+    p15, p15f = A("pc", 1, 2), A("pf", 3, 4)
+    r15, odd16 = A("ri", 64, 80), A("hs", 48, 64)
     ts(p15, A("pc", 0, 1), 15, Op.bitwise_and)
+    ts(r15, A("ri", 0, 16), 15, Op.bitwise_and)
+    ts(A("ri", 48, 64), A("ri", 32, 48), 1, Op.bitwise_and)
+    copy("V", p15f, p15)
+    ts(A("hs", 0, 16), r15, 0.0, Op.is_equal, -BIG, Op.mult)
+    ts(A("hs", 16, 32), r15, 1.0, Op.is_equal, K, Op.mult)
+    copy("V", odd16, A("ri", 48, 64))
+    ts(A("tu", 0, 28), A("ci", 0, 28), 0.0, Op.mult, p15f, Op.add)
+    tt(A("hs", 32, 48), A("hs", 0, 16), A("hs", 16, 32), Op.add)
     ts(kc, p15, 15.0, Op.is_lt, K, Op.mult)
-    ts(A("pf", 2, 3), p15, 15.0, Op.is_lt, 2.0, Op.mult)
-    ts(thr, A("pf", 2, 3), 0.5, Op.add)
-    copy("V", A("pf", 3, 4), p15)
-    ts(cl, A("ci", 0, 28), A("pf", 3, 4), Op.add)
-    ts(ck, cl, kc, Op.add)
+    ts(kb, p15, 15.0, Op.is_lt, 2.0, Op.mult)
+    ts(cl, A("ci", 0, 28), p15f, Op.add)
     ts(A("pk", 8, 16), A("pk", 0, 8), 127, Op.bitwise_and)
+    ts(kc1, kc, -1.0, Op.add)
+    ts(ck, cl, kc, Op.add)
     copy("V", A("pu", 0, 8), A("pk", 8, 16))
     copy("V", A("pu", 16, 24), A("pk", 16, 24))
     copy("V", A("pu", 32, 40), A("pk", 32, 40))
+    hold16 = A("hs", 32, 48)
+    copy("S", A("hh", 0, C), ind(hold16, A("tu", 0, 28)))
+    copy("S", A("hb", 0, C), ind(hold16, A("tu", 0, 28)), 1.0 / 256)
+    copy("S", A("hf", 0, C), ind(hold16, A("tu", 0, 28)))
+    copy("S", A("par", 0, C), ind(odd16, A("tu", 0, 28)))
 
-    copy("V", A("nu2", 0, 56), A("nl2", 0, 56))
     ts(A("nb2", 0, 56), A("nl2", 0, 56), 1, Op.bitwise_and)
+    copy("V", A("nu2", 0, 56), A("nl2", 0, 56))
     ts(A("nw2", 0, 56), A("nb2", 0, 56), -2.0, Op.mult, 1.0, Op.add)
     tt(A("nx2", 0, 56), A("nl2", 0, 56), A("nw2", 0, 56), Op.add)
     copy("V", A("nxu2", 0, 56), A("nx2", 0, 56))
-    r15 = A("ri", C, 2 * C)
-    iot = A("iot", 0, C)
-    ixs = new("rows")
-    scat = ind(at(ixs, 0, C), A("nxu2", 28, 56))
-    emit("V", lambda e: e.tensor_copy(scat[0], iot[0]), [at(ixs, 0, C)], [iot, A("nxu2", 28, 56)])
-    ix0 = new("rows")
-    scat0 = ind(at(ix0, 0, C), A("nxu2", 0, 28))
-    emit("V", lambda e: e.tensor_copy(scat0[0], iot[0]), [at(ix0, 0, C)], [iot, A("nxu2", 0, 28)])
-    drs = new("rows")
+
+    def others(out, nx):
+        o, i = at(out, 0, C), A("iot", 0, C)
+        w = ind(o, nx)
+        emit("V", lambda e: e.tensor_copy(w[0], i[0]), [o], [i, nx])
+
+    ixs, ix0, drs = new("rows"), new("rows"), new("hr")
+    others(ixs, A("nxu2", 28, 56))
     gather("S", drs, ixs, ("nu2", 28))
-    ts(r15, A("ri", 0, C), 15, Op.bitwise_and)
-    ts(A("hf", 0, C), r15, 0.0, Op.is_equal, -BIG, Op.mult)
-    ts(A("hf", C, 2 * C), r15, 1.0, Op.is_equal, K, Op.mult)
-    tt(A("hf", 0, C), A("hf", 0, C), A("hf", C, 2 * C), Op.add)
-    ts(A("hb", 0, C), A("hf", 0, C), 1.0 / 256, Op.mult)
-    nrow, drow = new("rows"), new("rows")
-    gather("S", drow, ix0, ("nu2", 0))
-    gather("S", nrow, IOT, ("nu2", 0))
-    odd = new("lf")
-    copy("V", at(odd, 0, 28), A("nb2", 28, 56))
-
-    def even_ends(v, odd, out):
-        t, h = new("lf"), new("lf")
-        tt(out, v, ck, Op.subtract)
-        tt(at(t, 0, 28), at(odd, 0, 28), out, Op.mult)
-        return t, h
-    v = scan(drs)
-    dd = new("lf")
-    t, h = even_ends(v, odd, at(dd, 0, 28))
-    tt(at(h, 0, 28), at(t, 0, 28), cl, Op.add)
-    hu = new("lu")
-    copy("V", at(hu, 0, 28), at(h, 0, 28))
-
     quant("uq", "us", 0, 128, A("ut", 0, 512))
-    for k in range(3):
+
+    def side(k):
         off = A("pu", 16 * k, 16 * k + 8)
-        o = A("pq", 128 * k, 128 * k + 128, bits=dt.uint32)
-        w = ind(A("uq", 0, 128, bits=dt.uint32), off)
-        emit("V", lambda e: e.tensor_copy(o[0], w[0]), [o], [w])
-        o2, w2 = A("ps", 128 * k, 128 * k + 128), ind(A("us", 0, 128), off)
-        emit("V", lambda e: e.tensor_copy(o2[0], w2[0]), [o2], [w2])
+        o, w = A("pq", 128 * k, 128 * k + 128, bits=dt.uint32), ind(A("uq", 0, 128, bits=dt.uint32), off)
+        copy("V", o, w)
+        copy("S", A("ps", 128 * k, 128 * k + 128), ind(A("us", 0, 128), off))
 
     half = [(0, H), (H, C)]
 
@@ -315,163 +296,200 @@ def rank_program(g, core, T, topo):
         a, b = half[k]
         quant("xq", "xs", a, b, A("xt", 4 * a, 4 * b))
 
-    def scores(k):
-        a, b = half[k]
-        banks = [3, 4, 5] if k == 0 else [0, 1, 2]
-        for j in range(3):
-            mm(banks[j], "pq", "ps", 128 * j, "xq", "xs", a, b)
-        for j in range(3):
-            o, i = A("fl", C * j + a, C * j + b), bank(banks[j])
-            if j == 0: ts(o, i, 0.0, Op.is_gt)
-            else: emit("S", lambda e: e.activation(o[0], i[0], Act.Sign), [o], [i])
+    banks = [[3, 4, 5], [0, 1, 2]]
 
-    def planes(rd, k):
+    def scores(k, js=(0, 1, 2)):
+        for j in js:
+            mm(banks[k][j], "pq", "ps", 128 * j, "xq", "xs", half[k][0], half[k][1])
+
+    def signs(k, js=(0, 1, 2)):
+        for j in js:
+            o, i = A("fl", C * j + half[k][0], C * j + half[k][1]), bank(banks[k][j])
+            if j == 0 and k == 0: ts(o, i, 0.0, Op.is_gt)
+            else: act(o, i, Act.Sign)
+
+    side(0)
+    for k in (1, 0):
+        states(k)
+        scores(k, [0])
+    for k in (1, 0): signs(k, [0])
+    v = scan(drs)
+    dd, hu = A("shf", 0, 28), new("lu")
+    t, h, odd = new("lf"), new("lf"), new("lf")
+    copy("V", at(odd), A("nb2", 28, 56))
+    tt(dd, v, ck, Op.subtract)
+    tt(at(t), at(odd), dd, Op.mult)
+    tt(at(h), at(t), cl, Op.add)
+    copy("V", at(hu), at(h))
+    drow, nrow, prow = new("rows"), new("rows"), ("pr", 0)
+
+    def first():
+        others(ix0, A("nxu2", 0, 28))
+        gather("S", drow, ix0, ("nu2", 0))
+        side(1)
+        side(2)
+        memset(A("sg", 0, 128), 0.0)
+
+    def second():
+        gather("S", prow, ("par", 0), ("nu2", 0))
+        return offsets(scan(ix0))
+
+    def third():
+        gather("S", nrow, IOT, ("nu2", 0))
+        for k in (1, 0):
+            scores(k, [1, 2])
+            signs(k, [1])
+
+    one = A("one", 0, 512)
+    memset(one, 1.0)
+    for b in range(4):
+        et = A("et", 512 * b, 512 * b + 512)
+        emit("G", lambda e: e.affine_select(et[0], one[0], [[1, 512]], Op.is_equal, 0.0, -b, -4), [et], [one])
+
+    def planes(k):
         a, b = half[k]
         for e in range(4):
-            x = A("xt", 4 * a + e, 4 * b, 4)
-            copy("S", A("xh", 4 * C * (rd % 2) + C * e + a, 4 * C * (rd % 2) + C * e + b), x, 0.5)
+            copy("S", A("xh", C * e + a, C * e + b), A("xt", 4 * a + e, 4 * b, 4), 0.5)
 
     def planes32(k):
         a, b = half[k]
         for e in range(4):
             copy("S", A("xb", C * e + a, C * e + b), A("xt", 4 * a + e, 4 * b, 4), 32.0)
 
-    def shift(sig):
-        t1, t2, t3 = ("sg", 32), ("sg", 64), ("sg", 96)
+    def shift():
         i, o = A("sg", 0, 32), A("sg", 32, 64)
         emit("V", lambda e: e.transpose(o[0], i[0]), [o], [i])
-        copy("V", A("sg", 80, 96), A("sg", 32, 48))
         for a in range(4):
             d = 32 * ((a + 1) % 4)
             copy("S" if a in (1, 2) else "V", A("sg", 64, 80, p0=d, p1=d + 32), A("sg", 48, 64, p0=32 * a, p1=32 * a + 32))
+        copy("V", A("sg", 80, 96), A("sg", 32, 48))
         i2, o2 = A("sg", 64, 96), A("sg", 96, 128)
         emit("V", lambda e: e.transpose(o2[0], i2[0]), [o2], [i2])
         return A("sg", 96, 124)
 
-    states(1)
-    scores(1)
-    states(0)
-    scores(0)
-    planes(0, 1)
-    for b in range(4):
-        quant("eq", "es", 128 * b, 128 * b + 128, A("et", 512 * b, 512 * b + 512))
-    quant("vq", "vs", 0, 128, A("vi", 0, 512))
-
+    pending, others_list = [], None
     for rd, step in enumerate(STEP):
         last = rd == 2
         p, q = T.cores[(rank - step) % 4], T.cores[(rank + step) % 4]
+        np_, nq_ = len(topo.engines(core, p)), len(topo.engines(core, q))
+        later, late = pending, []
         for j in range(3):
             frow = new("fr")
-            both(frow, ("fl", C * j), hu)
-            F = flags(frow)
-            t = new("lf")
-            tt(at(t, 0, 28), at(F, 0, 28), at(dd, 0, 28), Op.mult)
-            su = new("lu")
-            if j == 0:
-                s = new("lf")
-                tt(at(s, 0, 28), at(t, 0, 28), cl, Op.add)
-                copy("V", at(su, 0, 28), at(s, 0, 28))
-            else:
-                tt(A("sg", 0, 28), at(t, 0, 28), cl, Op.add)
-                copy("V", at(su, 0, 28), shift(None))
-            n2 = new("rows")
-            if j == 2:
-                both(n2, nrow, su)
-                nrow = n2
-                break
-            srow, erow, d2 = new("rows"), new("rows"), new("rows")
+            act(at(frow, H, C), ind(A("fl", C * j, C * j + C), at(hu, 14, 28)), Act.Relu)
+            ts(at(frow, 0, H), ind(A("fl", C * j, C * j + C), at(hu, 0, 14)), 0.0, Op.max)
+            for fn in later: fn()
+            kd, base = new("lf"), new("lf")
+            ts(at(kd), dd, kb, Op.mult)
+            tt(at(base), cl, at(kd), Op.subtract)
+            v = scan(frow)
+            t, s, su = new("lf"), new("lf") if j == 0 else ("sg", 0), new("lu")
+            tt(at(t), v, dd, Op.mult)
+            tt(at(s), at(t), at(base), Op.add)
+            if j: copy("V", at(su), shift())
+            else: copy("V", at(su), at(s))
+            n2, srow = new("rows"), new("rows")
+            if j == 2: break
+            if rd == 0 and j == 0: first()
+            e1, p2, d2, xr = new("hr"), new("fr"), new("hr"), new("hr")
+            both(e1, drow, su)
             gather("S", srow, IOT, su)
-            gather("V", erow, drow, su)
+            eu = offsets(scan(e1))
+            if rd == 0 and j == 0: others_list = second()
+            for fn in late: fn()
+            gather("S", p2, prow, su)
+            gather("V", d2, srow, eu)
+            if rd == 0 and j == 0: third()
             gather("S", n2, nrow, su)
-            v = scan(erow)
-            eu = new("lu")
-            ts(at(eu, 0, 28), v, kc, Op.subtract)
-            both(d2, srow, eu)
-            nv = scan(n2)
-            ni, nb, odd = new("li"), new("li"), new("lf")
-            ts(at(ni, 0, 28), nv, kc, Op.subtract)
-            ts(at(nb, 0, 28), at(ni, 0, 28), 1, Op.bitwise_and)
-            copy("V", at(odd, 0, 28), at(nb, 0, 28))
+            gather("S", xr, srow, others_list)
+            pv = scan(p2)
             v = scan(d2)
-            dd = new("lf")
-            t, h = even_ends(v, odd, at(dd, 0, 28))
-            tt(at(h, 0, 28), at(t, 0, 28), cl, Op.add)
-            hu = new("lu")
-            copy("V", at(hu, 0, 28), at(h, 0, 28))
-            nrow, drow = n2, d2
-        nu = ("req", 32 * rd)
-        va = scan(nrow, 0, H)
-        ts(at(nu, 0, 14), va, kc, Op.subtract)
+            odd, dl, t, h, hu = new("lf"), new("lf"), new("lf"), new("lf"), new("lu")
+            ts(at(odd), pv, kb, Op.subtract)
+            dd = at(dl)
+            tt(dd, v, ck, Op.subtract)
+            tt(at(t), at(odd), dd, Op.mult)
+            tt(at(h), at(t), cl, Op.add)
+            copy("V", at(hu), at(h))
+            nrow, prow, others_list = n2, p2, new("lu")
+            later, late = [], [lambda xr=xr, lu=others_list: offsets(scan(xr), lu)]
+            if j == 0:
+                drow = new("rows")
+                later.append(lambda drow=drow, srow=srow, eu=eu: gather("S", drow, srow, eu))
+                if rd == 0: later.append(lambda: [signs(k, [2]) for k in (1, 0)])
+        nh, no, nu = new("hr"), new("hr"), ("req", 32 * rd)
+        gather("S", srow, IOT, su)
+        gather("V", nh, nrow, su, 0, H)
+        offsets(scan(nh, 0, H, no), nu, 0, 14)
         remote(p, A("lreq", 32 * rd, 32 * rd + 14), at(nu, 0, 14), "rr%d" % rd, "kr%d" % rd)
-        vb = scan(nrow, H, C)
-        ts(at(nu, 14, 28), vb, kc, Op.subtract)
-        ni, nb, nw, nx, nxu = new("li"), new("li"), new("li"), new("li"), new("lu")
-        copy("V", at(ni, 0, 28), at(nu, 0, 28))
-        ts(at(nb, 0, 28), at(ni, 0, 28), 1, Op.bitwise_and)
-        ts(at(nw, 0, 28), at(nb, 0, 28), -2.0, Op.mult, 1.0, Op.add)
-        tt(at(nx, 0, 28), at(ni, 0, 28), at(nw, 0, 28), Op.add)
-        copy("V", at(nxu, 0, 28), at(nx, 0, 28))
+        for fn in late: fn()
         ix = new("rows")
-        sc = ind(at(ix, 0, C), at(nxu, 0, 28))
-        emit("V", lambda e: e.tensor_copy(sc[0], iot[0]), [at(ix, 0, C)], [iot, at(nxu, 0, 28)])
-        planes(rd, 0)
-        vi = scan(ix)
+        both(ix, srow, others_list)
         iu = ("inv", 32 * rd)
-        ts(at(iu, 0, 28), vi, kc, Op.subtract)
-        remote(q, A("linv", 32 * rd, 32 * rd + 28), at(iu, 0, 28), "ri%d" % rd, "ki%d" % rd)
+        offsets(scan(ix), iu)
+        remote(q, A("linv", 32 * rd, 32 * rd + 28), at(iu), "ri%d" % rd, "ki%d" % rd)
+        others_list = iu
+        planes(1)
+        planes(0)
+        gather("V", nh, nrow, su, H, C)
+        offsets(scan(nh, H, C, no), nu, 14, 28)
+        nv = at(no, 15, C, 16)
+        n2i, n1, b2, nx, nxu = new("li"), new("li"), new("li"), new("li"), new("lu")
+        ts(at(n2i), nv, kc, Op.subtract, 2.0, Op.mult)
+        ts(at(n1), nv, kc1, Op.subtract)
+        ts(at(b2), at(n2i), 2, Op.bitwise_and)
+        tt(at(nx), at(n1), at(b2), Op.subtract)
+        copy("V", at(nxu), at(nx))
+        arrive([A("lreq", 32 * rd, 32 * rd + 14)], "rr%d" % rd, nq_)
+        nq = ("lreq", 32 * rd)
+        for e in range(4):
+            gather("S", ("za", H * e), ("xh", C * e), nq, 0, H)
+        gather("S", n2, nrow, su)
+        nrow = n2
         if last:
             dma("Y", (T.nm[:, :], []), A("rows", nrow[1], nrow[1] + C, pstep=16))
-        nen = len(topo.engines(core, q))
-        arrive([A("lreq", 32 * rd, 32 * rd + 14)], "rr%d" % rd, nen)
-        nq = ("lreq", 32 * rd)
-        X = [("xh", 4 * C * (rd % 2) + C * e) for e in range(4)]
-        for e in range(4):
-            gather("S", ("za", H * e), X[e], nq, 0, H)
-        brow = new("rows")
+        brow = new("hr")
         gather("V", brow, ix, nq, 0, H)
-        bv = scan(brow, 0, H)
-        bu = new("lu")
-        ts(at(bu, 0, 14), bv, kc, Op.subtract)
-        for e in range(4):
-            tt(A("zt", e, 4 * H, 4), ind(at(X[e], 0, C), at(bu, 0, 14)), A("za", H * e, H * e + H), Op.add)
-        zc, zp = A("zq", H * rd, H * rd + H), A("zs", H * rd, H * rd + H)
-        zt = A("zt", 0, 4 * H)
-        emit("V", lambda e: e.quantize_mx(zc[0], zp[0], zt[0]), [zc, zp], [zt])
+        bu = offsets(scan(brow, 0, H), None, 0, 14)
+
+        def means(out, step0, first_, lu, a):
+            for e in range(4):
+                tt(A(out, step0 + e, step0 + 4 * H, 4), ind(A("xh", C * e, C * e + C), at(lu, a, a + 14)), A("za", first_ + H * e, first_ + H * e + H), Op.add)
+        means("zt", 0, 0, bu, 0)
+        quant("zq", "zs", H * rd, H * rd + H, A("zt", 0, 4 * H))
         remote(q, A("lq", H * rd, H * rd + H, bits=dt.uint8), A("zq", H * rd, H * rd + H, bits=dt.uint8), "rc%d" % rd, "kc%d" % rd)
-        remote(q, A("ls", H * rd, H * rd + H), zp, "rc%d" % rd, "kc%d" % rd)
+        remote(q, A("ls", H * rd, H * rd + H), A("zs", H * rd, H * rd + H), "rc%d" % rd, "kc%d" % rd)
         drow = new("rows")
         gather("S", drow, ix, nu)
-        arrive([A("linv", 32 * rd, 32 * rd + 28)], "ri%d" % rd, len(topo.engines(core, p)))
-        ip, mrow = new("rows"), new("rows")
-        both(ip, IOT, ("linv", 32 * rd))
+        arrive([A("linv", 32 * rd, 32 * rd + 28)], "ri%d" % rd, np_)
+        ip, mrow, er, dr = new("rows"), new("hr"), new("hr"), new("hr")
+        gather("S", ip, IOT, ("linv", 32 * rd))
+        if not last:
+            odd, t, w = new("lf"), new("lf"), 64 * rd
+            v = scan(drow)
+            copy("V", at(odd), at(b2), 0.5)
+            tt(A("own", w, w + 28), v, ck, Op.subtract)
+            tt(at(t), at(odd), A("own", w, w + 28), Op.mult)
+            tt(A("own", w + 28, w + 56), at(t), cl, Op.add)
+            dma("Y", A("shf", w, w + 56, p0=16), A("own", w, w + 56, p0=0, p1=112))
+            dma("Y", A("shf", w, w + 56, p0=0, p1=16), A("own", w, w + 56, p0=112, p1=128))
         both(mrow, ip, nxu, H, C)
-        mv = scan(mrow, H, C)
-        mu = new("lu")
-        ts(at(mu, 14, 28), mv, kc, Op.subtract)
-        er, dr = new("rows"), new("rows")
+        mu = offsets(scan(mrow, H, C), None, 14, 28)
         gather("S", er, nrow, mu, H, C)
         gather("V", dr, drow, mu, H, C)
-        ev = scan(er, H, C)
-        eu, du = new("lu"), new("lu")
-        ts(at(eu, 14, 28), ev, kc, Op.subtract)
+        du = offsets(scan(dr, H, C), None, 14, 28)
+        eu = offsets(scan(er, H, C), None, 14, 28)
         for e in range(4):
-            copy("S", A("za", 4 * H + H * e, 4 * H + H * e + H), ind(at(X[e], 0, C), at(eu, 14, 28)))
-        dv = scan(dr, H, C)
-        ts(at(du, 14, 28), dv, kc, Op.subtract)
-        if rd == 0: planes32(1)
-        for e in range(4):
-            tt(A("vt", 4 * H + e, 4 * C, 4), ind(at(X[e], 0, C), at(du, 14, 28)), A("za", 4 * H + H * e, 4 * H + H * e + H), Op.add)
+            copy("S", A("za", 4 * H + H * e, 4 * H + H * e + H), ind(A("xh", C * e, C * e + C), at(eu, 14, 28)))
+        planes32(1)
+        planes32(0)
+        means("vt", 4 * H, 4 * H, du, 14)
         quant("mq", "ms", H, C, A("vt", 4 * H, 4 * C))
         for e in range(4):
             mm(e, "wq", "wp", 128 * e, "mq", "ms", H, C)
-        if not last:
-            v = scan(drow)
-            odd = new("lf")
-            copy("V", at(odd, 0, 28), at(nb, 0, 28))
-            t, h = even_ends(v, odd, A("own", 0, 28))
-            tt(A("own", 28, 56), at(t, 0, 28), cl, Op.add)
-            dma("Y", A("shf", 0, 56, p0=16), A("own", 0, 56, p0=0, p1=112))
-            dma("Y", A("shf", 0, 56, p0=0, p1=16), A("own", 0, 56, p0=112, p1=128))
+        if rd == 0:
+            for b in range(4):
+                quant("eq", "es", 128 * b, 128 * b + 128, A("et", 512 * b, 512 * b + 512))
+            quant("vq", "vs", 0, 128, A("vi", 0, 512))
 
         def new_state(k, banks):
             a, b = half[k]
@@ -479,7 +497,6 @@ def rank_program(g, core, T, topo):
                 o = A("tmp", C * e + a, C * e + b)
                 tt(o, bank(banks[e]), A("xb", C * e + a, C * e + b), Op.add)
                 copy("S", A("xt", 4 * a + e, 4 * b, 4), o, 0.03125)
-            states(k)
 
         def finish(k):
             a, b = half[k]
@@ -491,16 +508,8 @@ def rank_program(g, core, T, topo):
             copy("V", A("yo", a, b), bank(bk))
             dma("Y", (T.y[:, a:b], []), A("yo", a, b))
 
-        planes32(0)
         new_state(1, [0, 1, 2, 3])
-        if last: finish(1)
-        else:
-            scores(1)
-            planes(rd + 1, 1)
-            planes32(1)
-            dd, hu = ("shf", 0), new("lu")
-            copy("V", at(hu, 0, 28), A("shf", 28, 56))
-        arrive([A("lq", H * rd, H * rd + H), A("ls", H * rd, H * rd + H)], "rc%d" % rd, 2 * len(topo.engines(core, p)))
+        arrive([A("lq", H * rd, H * rd + H), A("ls", H * rd, H * rd + H)], "rc%d" % rd, 2 * np_)
         for e in range(4):
             mm(4 + e, "eq", "es", 128 * e, "lq", "ls", H * rd, H * rd + H)
         for e in range(4):
@@ -508,9 +517,21 @@ def rank_program(g, core, T, topo):
         quant("mq", "ms", 0, H, A("vt", 0, 4 * H))
         for e in range(4):
             mm(4 + e, "wq", "wp", 128 * e, "mq", "ms", 0, H)
+        states(1)
+        if last: finish(1)
+        else: scores(1)
         new_state(0, [4, 5, 6, 7])
-        if last: finish(0)
-        else: scores(0)
+        states(0)
+        if last:
+            finish(0)
+            break
+        scores(0)
+        dd, hu, prow = A("shf", w, w + 28), new("lu"), ("pr", C * (rd + 1))
+        copy("V", at(hu), A("shf", w + 28, w + 56))
+        signs(0, [0])
+        signs(1)
+        signs(0, [1, 2])
+        pending = [lambda prow=prow, nu=nu: gather("S", prow, ("par", 0), nu)]
 
     for s in sorted(total):
         if clock["G"].get(s, 0) < total[s]:

@@ -27,7 +27,7 @@ SCRATCH = {
     "zq": ("sbuf", [128, 3 * H], "float8_e4m3fn_x4"), "zs": ("sbuf", [128, 3 * H], "uint8"),
     "lq": ("sbuf", [128, 3 * H], "float8_e4m3fn_x4"), "ls": ("sbuf", [128, 3 * H], "uint8"),
     "mq": ("sbuf", [128, C], "float8_e4m3fn_x4"), "ms": ("sbuf", [128, C], "uint8"),
-    "rows": ("sbuf", [128, NROW * C], "float32"), "hr": ("sbuf", [128, NHALF * C], "float16"), "fr": ("sbuf", [128, NSIGN * C], "bfloat16"),
+    "rows": ("sbuf", [128, NROW * C], "bfloat16"), "nmo": ("sbuf", [128, C], "float32"), "hr": ("sbuf", [128, NHALF * C], "float16"), "fr": ("sbuf", [128, NSIGN * C], "bfloat16"),
     "lf": ("sbuf", [128, NLIST * 32], "float32"),
     "lu": ("sbuf", [128, NLIST * 32], "uint16"),
     "li": ("sbuf", [128, NLIST * 32], "int32"),
@@ -40,8 +40,8 @@ SCRATCH = {
     "sg": ("sbuf", [128, 128], "float32"),
     "req": ("sbuf", [128, 3 * 32], "uint16"), "inv": ("sbuf", [128, 3 * 32], "uint16"),
     "lreq": ("sbuf", [128, 3 * 32], "uint16"), "linv": ("sbuf", [128, 3 * 32], "uint16"),
-    "iot": ("sbuf", [128, C], "float32"), "par": ("sbuf", [128, C], "bfloat16"),
-    "hf": ("sbuf", [128, C], "float32"), "hh": ("sbuf", [128, C], "float16"), "hb": ("sbuf", [128, C], "bfloat16"),
+    "iot": ("sbuf", [128, C], "bfloat16"), "par": ("sbuf", [128, C], "bfloat16"),
+    "hh": ("sbuf", [128, C], "float16"), "hb": ("sbuf", [128, C], "bfloat16"),
     "hs": ("sbuf", [128, 96], "float32"), "ri": ("sbuf", [128, 96], "int32"), "tu": ("sbuf", [128, 32], "uint16"),
     "pc": ("sbuf", [128, 8], "int32"), "pf": ("sbuf", [128, 8], "float32"),
     "ci": ("sbuf", [128, 32], "int32"), "cl": ("sbuf", [128, 64], "float32"),
@@ -195,8 +195,8 @@ def rank_program(g, core, T, topo):
         gather("V", out, win, lu, a, a + h)
 
     def scan(row, a=0, b=C, o=None):
-        o = o or new(row[0])
-        hold, r, out = A({"rows": "hf", "hr": "hh", "fr": "hb"}[row[0]], 0, b - a), at(row, a, b), at(o, a, b)
+        o = o or new("hr" if row[0] == "rows" else "fr")
+        hold, r, out = A("hh" if row[0] == "rows" else "hb", 0, b - a), at(row, a, b), at(o, a, b)
         emit("V", lambda e: e.tensor_tensor_scan(out[0], hold[0], r[0], 0.0, Op.add, Op.max), [out], [hold, r])
         return at(o, a + 15, b, 16)
 
@@ -238,7 +238,7 @@ def rank_program(g, core, T, topo):
     iota(A("ci", 0, 28), [[16, 28]], 0, 0)
     iota(A("ri", 0, 16), [[1, 16]], 128, -1)
     iota(A("ri", 32, 48), [[1, 16]], 0, 0)
-    iota(A("iot", 0, C), [[1, C]], 0, 0, True)
+    iota(A("iot", 0, C), [[1, C]], -H, 0, True)
     iota(A("pk", 0, 8), [[16, 8]], 112, 0)
     iota(A("pk", 16, 24), [[16, 8]], 1, 0)
     iota(A("pk", 32, 40), [[16, 8]], 2, 0)
@@ -253,19 +253,12 @@ def rank_program(g, core, T, topo):
     copy("V", odd16, A("ri", 48, 64))
     ts(A("tu", 0, 28), A("ci", 0, 28), 0.0, Op.mult, p15f, Op.add)
     tt(A("hs", 32, 48), A("hs", 0, 16), A("hs", 16, 32), Op.add)
-    ts(kc, p15, 15.0, Op.is_lt, K, Op.mult)
+    ts(A("pf", 4, 5), p15, 15.0, Op.is_lt, K, Op.mult)
     ts(kb, p15, 15.0, Op.is_lt, 2.0, Op.mult)
-    ts(cl, A("ci", 0, 28), p15f, Op.add)
-    ts(A("pk", 8, 16), A("pk", 0, 8), 127, Op.bitwise_and)
-    ts(kc1, kc, -1.0, Op.add)
-    ts(ck, cl, kc, Op.add)
-    copy("V", A("pu", 0, 8), A("pk", 8, 16))
-    copy("V", A("pu", 16, 24), A("pk", 16, 24))
-    copy("V", A("pu", 32, 40), A("pk", 32, 40))
+    ts(kc, A("pf", 4, 5), -float(H), Op.add)
     hold16 = A("hs", 32, 48)
     copy("S", A("hh", 0, C), ind(hold16, A("tu", 0, 28)))
     copy("S", A("hb", 0, C), ind(hold16, A("tu", 0, 28)), 1.0 / 256)
-    copy("S", A("hf", 0, C), ind(hold16, A("tu", 0, 28)))
     copy("S", A("par", 0, C), ind(odd16, A("tu", 0, 28)))
 
     ts(A("nb2", 0, 56), A("nl2", 0, 56), 1, Op.bitwise_and)
@@ -279,9 +272,18 @@ def rank_program(g, core, T, topo):
         w = ind(o, nx)
         emit("V", lambda e: e.tensor_copy(w[0], i[0]), [o], [i, nx])
 
-    ixs, ix0, drs = new("rows"), new("rows"), new("hr")
+    ixs, ix0, drs, drow, nrow, prow = new("rows"), new("rows"), new("rows"), new("rows"), new("rows"), ("pr", 0)
     others(ixs, A("nxu2", 28, 56))
+    gather("S", nrow, IOT, ("nu2", 0))
+    gather("S", prow, ("par", 0), ("nu2", 0))
     gather("S", drs, ixs, ("nu2", 28))
+    ts(cl, A("ci", 0, 28), p15f, Op.add)
+    ts(A("pk", 8, 16), A("pk", 0, 8), 127, Op.bitwise_and)
+    ts(kc1, kc, -1.0, Op.add)
+    ts(ck, cl, kc, Op.add)
+    copy("V", A("pu", 0, 8), A("pk", 8, 16))
+    copy("V", A("pu", 16, 24), A("pk", 16, 24))
+    copy("V", A("pu", 32, 40), A("pk", 32, 40))
     quant("uq", "us", 0, 128, A("ut", 0, 512))
 
     def side(k):
@@ -308,37 +310,38 @@ def rank_program(g, core, T, topo):
             if j == 0 and k == 0: ts(o, i, 0.0, Op.is_gt)
             else: act(o, i, Act.Sign)
 
+    def pairs(v, odd):
+        t, kd, h, dd, base, hu = new("lf"), new("lf"), new("lf"), new("lf"), new("lf"), new("lu")
+        tt(at(dd), v, ck, Op.subtract)
+        tt(at(t), at(odd), at(dd), Op.mult)
+        ts(at(kd), at(dd), kb, Op.mult)
+        tt(at(h), at(t), cl, Op.add)
+        tt(at(base), cl, at(kd), Op.subtract)
+        copy("V", at(hu), at(h))
+        return at(dd), at(base), hu
+
     side(0)
     for k in (1, 0):
         states(k)
         scores(k, [0])
+    others(ix0, A("nxu2", 0, 28))
+    gather("S", drow, ix0, ("nu2", 0))
     for k in (1, 0): signs(k, [0])
     v = scan(drs)
-    dd, hu = A("shf", 0, 28), new("lu")
-    t, h, odd = new("lf"), new("lf"), new("lf")
+    odd = new("lf")
     copy("V", at(odd), A("nb2", 28, 56))
-    tt(dd, v, ck, Op.subtract)
-    tt(at(t), at(odd), dd, Op.mult)
-    tt(at(h), at(t), cl, Op.add)
-    copy("V", at(hu), at(h))
-    drow, nrow, prow = new("rows"), new("rows"), ("pr", 0)
-
-    def first():
-        others(ix0, A("nxu2", 0, 28))
-        gather("S", drow, ix0, ("nu2", 0))
-        side(1)
-        side(2)
-        memset(A("sg", 0, 128), 0.0)
+    dd, base, hu = pairs(v, odd)
 
     def second():
-        gather("S", prow, ("par", 0), ("nu2", 0))
+        side(1)
+        side(2)
         return offsets(scan(ix0))
 
     def third():
-        gather("S", nrow, IOT, ("nu2", 0))
         for k in (1, 0):
             scores(k, [1, 2])
             signs(k, [1])
+        memset(A("sg", 0, 128), 0.0)
 
     one = A("one", 0, 512)
     memset(one, 1.0)
@@ -346,9 +349,9 @@ def rank_program(g, core, T, topo):
         et = A("et", 512 * b, 512 * b + 512)
         emit("G", lambda e: e.affine_select(et[0], one[0], [[1, 512]], Op.is_equal, 0.0, -b, -4), [et], [one])
 
-    def planes(k):
+    def planes(k, es=(0, 1, 2, 3)):
         a, b = half[k]
-        for e in range(4):
+        for e in es:
             copy("S", A("xh", C * e + a, C * e + b), A("xt", 4 * a + e, 4 * b, 4), 0.5)
 
     def planes32(k):
@@ -357,13 +360,12 @@ def rank_program(g, core, T, topo):
             copy("S", A("xb", C * e + a, C * e + b), A("xt", 4 * a + e, 4 * b, 4), 32.0)
 
     def shift():
-        i, o = A("sg", 0, 32), A("sg", 32, 64)
+        i, o = A("sg", 0, 32), A("sg", 48, 80)
         emit("V", lambda e: e.transpose(o[0], i[0]), [o], [i])
         for a in range(4):
             d = 32 * ((a + 1) % 4)
-            copy("S" if a in (1, 2) else "V", A("sg", 64, 80, p0=d, p1=d + 32), A("sg", 48, 64, p0=32 * a, p1=32 * a + 32))
-        copy("V", A("sg", 80, 96), A("sg", 32, 48))
-        i2, o2 = A("sg", 64, 96), A("sg", 96, 128)
+            copy("S" if a in (1, 2) else "V", A("sg", 32, 48, p0=d, p1=d + 32), A("sg", 64, 80, p0=32 * a, p1=32 * a + 32))
+        i2, o2 = A("sg", 32, 64), A("sg", 96, 128)
         emit("V", lambda e: e.transpose(o2[0], i2[0]), [o2], [i2])
         return A("sg", 96, 124)
 
@@ -378,76 +380,62 @@ def rank_program(g, core, T, topo):
             act(at(frow, H, C), ind(A("fl", C * j, C * j + C), at(hu, 14, 28)), Act.Relu)
             ts(at(frow, 0, H), ind(A("fl", C * j, C * j + C), at(hu, 0, 14)), 0.0, Op.max)
             for fn in later: fn()
-            kd, base = new("lf"), new("lf")
-            ts(at(kd), dd, kb, Op.mult)
-            tt(at(base), cl, at(kd), Op.subtract)
             v = scan(frow)
             t, s, su = new("lf"), new("lf") if j == 0 else ("sg", 0), new("lu")
             tt(at(t), v, dd, Op.mult)
-            tt(at(s), at(t), at(base), Op.add)
+            tt(at(s), at(t), base, Op.add)
             if j: copy("V", at(su), shift())
             else: copy("V", at(su), at(s))
             n2, srow = new("rows"), new("rows")
             if j == 2: break
-            if rd == 0 and j == 0: first()
-            e1, p2, d2, xr = new("hr"), new("fr"), new("hr"), new("hr")
+            e1, p2, d2, xr = new("rows"), new("fr"), new("rows"), new("rows")
             both(e1, drow, su)
             gather("S", srow, IOT, su)
             eu = offsets(scan(e1))
-            if rd == 0 and j == 0: others_list = second()
+            gather("V", p2, prow, su)
+            gather("S", d2, srow, eu)
+            if rd == 0 and j == 0:
+                others_list = second()
+                third()
             for fn in late: fn()
-            gather("S", p2, prow, su)
-            gather("V", d2, srow, eu)
-            if rd == 0 and j == 0: third()
             gather("S", n2, nrow, su)
-            gather("S", xr, srow, others_list)
+            if j == 1: planes(1)
+            elif rd: planes(0, (0, 1))
             pv = scan(p2)
             v = scan(d2)
-            odd, dl, t, h, hu = new("lf"), new("lf"), new("lf"), new("lf"), new("lu")
+            odd = new("lf")
             ts(at(odd), pv, kb, Op.subtract)
-            dd = at(dl)
-            tt(dd, v, ck, Op.subtract)
-            tt(at(t), at(odd), dd, Op.mult)
-            tt(at(h), at(t), cl, Op.add)
-            copy("V", at(hu), at(h))
-            nrow, prow, others_list = n2, p2, new("lu")
-            later, late = [], [lambda xr=xr, lu=others_list: offsets(scan(xr), lu)]
-            if j == 0:
-                drow = new("rows")
-                later.append(lambda drow=drow, srow=srow, eu=eu: gather("S", drow, srow, eu))
-                if rd == 0: later.append(lambda: [signs(k, [2]) for k in (1, 0)])
-        nh, no, nu = new("hr"), new("hr"), ("req", 32 * rd)
+            dd, base, hu = pairs(v, odd)
+            drow, nrow, prow, xl, others_list = d2, n2, p2, others_list, new("lu")
+            later = [lambda xr=xr, srow=srow, xl=xl: gather("S", xr, srow, xl)]
+            late = [lambda xr=xr, lu=others_list: offsets(scan(xr), lu)]
+            if rd == 0 and j == 0: later.append(lambda: [signs(k, [2]) for k in (1, 0)])
+        no, nu = new("hr"), ("req", 32 * rd)
         gather("S", srow, IOT, su)
-        gather("V", nh, nrow, su, 0, H)
-        offsets(scan(nh, 0, H, no), nu, 0, 14)
+        gather("V", n2, nrow, su, 0, H)
+        offsets(scan(n2, 0, H, no), nu, 0, 14)
         remote(p, A("lreq", 32 * rd, 32 * rd + 14), at(nu, 0, 14), "rr%d" % rd, "kr%d" % rd)
         for fn in late: fn()
         ix = new("rows")
+        gather("S", n2, nrow, su, H, C)
+        nrow = n2
         both(ix, srow, others_list)
         iu = ("inv", 32 * rd)
         offsets(scan(ix), iu)
         remote(q, A("linv", 32 * rd, 32 * rd + 28), at(iu), "ri%d" % rd, "ki%d" % rd)
         others_list = iu
-        planes(1)
-        planes(0)
-        gather("V", nh, nrow, su, H, C)
-        offsets(scan(nh, H, C, no), nu, 14, 28)
+        planes(0, (0, 1, 2, 3) if rd == 0 else (2, 3))
+        offsets(scan(nrow, H, C, no), nu, 14, 28)
         nv = at(no, 15, C, 16)
         n2i, n1, b2, nx, nxu = new("li"), new("li"), new("li"), new("li"), new("lu")
         ts(at(n2i), nv, kc, Op.subtract, 2.0, Op.mult)
         ts(at(n1), nv, kc1, Op.subtract)
         ts(at(b2), at(n2i), 2, Op.bitwise_and)
-        tt(at(nx), at(n1), at(b2), Op.subtract)
-        copy("V", at(nxu), at(nx))
         arrive([A("lreq", 32 * rd, 32 * rd + 14)], "rr%d" % rd, nq_)
         nq = ("lreq", 32 * rd)
         for e in range(4):
             gather("S", ("za", H * e), ("xh", C * e), nq, 0, H)
-        gather("S", n2, nrow, su)
-        nrow = n2
-        if last:
-            dma("Y", (T.nm[:, :], []), A("rows", nrow[1], nrow[1] + C, pstep=16))
-        brow = new("hr")
+        brow = new("rows")
         gather("V", brow, ix, nq, 0, H)
         bu = offsets(scan(brow, 0, H), None, 0, 14)
 
@@ -458,26 +446,21 @@ def rank_program(g, core, T, topo):
         quant("zq", "zs", H * rd, H * rd + H, A("zt", 0, 4 * H))
         remote(q, A("lq", H * rd, H * rd + H, bits=dt.uint8), A("zq", H * rd, H * rd + H, bits=dt.uint8), "rc%d" % rd, "kc%d" % rd)
         remote(q, A("ls", H * rd, H * rd + H), A("zs", H * rd, H * rd + H), "rc%d" % rd, "kc%d" % rd)
-        drow = new("rows")
-        gather("S", drow, ix, nu)
         arrive([A("linv", 32 * rd, 32 * rd + 28)], "ri%d" % rd, np_)
-        ip, mrow, er, dr = new("rows"), new("hr"), new("hr"), new("hr")
+        drow, ip, mrow, er, dr = new("rows"), new("rows"), new("rows"), new("rows"), new("rows")
         gather("S", ip, IOT, ("linv", 32 * rd))
+        tt(at(nx), at(n1), at(b2), Op.subtract)
         if not last:
-            odd, t, w = new("lf"), new("lf"), 64 * rd
-            v = scan(drow)
+            odd = new("lf")
             copy("V", at(odd), at(b2), 0.5)
-            tt(A("own", w, w + 28), v, ck, Op.subtract)
-            tt(at(t), at(odd), A("own", w, w + 28), Op.mult)
-            tt(A("own", w + 28, w + 56), at(t), cl, Op.add)
-            dma("Y", A("shf", w, w + 56, p0=16), A("own", w, w + 56, p0=0, p1=112))
-            dma("Y", A("shf", w, w + 56, p0=0, p1=16), A("own", w, w + 56, p0=112, p1=128))
+        copy("V", at(nxu), at(nx))
+        gather("S", drow, ix, nu)
         both(mrow, ip, nxu, H, C)
         mu = offsets(scan(mrow, H, C), None, 14, 28)
-        gather("S", er, nrow, mu, H, C)
-        gather("V", dr, drow, mu, H, C)
-        du = offsets(scan(dr, H, C), None, 14, 28)
+        gather("V", er, nrow, mu, H, C)
+        gather("S", dr, drow, mu, H, C)
         eu = offsets(scan(er, H, C), None, 14, 28)
+        du = offsets(scan(dr, H, C), None, 14, 28)
         for e in range(4):
             copy("S", A("za", 4 * H + H * e, 4 * H + H * e + H), ind(A("xh", C * e, C * e + C), at(eu, 14, 28)))
         planes32(1)
@@ -486,6 +469,14 @@ def rank_program(g, core, T, topo):
         quant("mq", "ms", H, C, A("vt", 4 * H, 4 * C))
         for e in range(4):
             mm(e, "wq", "wp", 128 * e, "mq", "ms", H, C)
+        if not last:
+            t, w = new("lf"), 64 * rd
+            v = scan(drow)
+            tt(A("own", w, w + 28), v, ck, Op.subtract)
+            tt(at(t), at(odd), A("own", w, w + 28), Op.mult)
+            tt(A("own", w + 28, w + 56), at(t), cl, Op.add)
+            dma("Y", A("shf", w, w + 56, p0=16), A("own", w, w + 56, p0=0, p1=112))
+            dma("Y", A("shf", w, w + 56, p0=0, p1=16), A("own", w, w + 56, p0=112, p1=128))
         if rd == 0:
             for b in range(4):
                 quant("eq", "es", 128 * b, 128 * b + 128, A("et", 512 * b, 512 * b + 512))
@@ -505,7 +496,7 @@ def rank_program(g, core, T, topo):
             dma("Y", (T.oc[:, 4 * a:4 * b], []), A("xq", a, b, bits=dt.uint8))
             for i in range(4):
                 dma("Y" if i % 2 else "S", (T.osc[4 * i:4 * i + 4, a:b], []), A("xs", a, b, p0=32 * i, p1=32 * i + 4))
-            copy("V", A("yo", a, b), bank(bk))
+            copy("S" if k else "V", A("yo", a, b), bank(bk))
             dma("Y", (T.y[:, a:b], []), A("yo", a, b))
 
         new_state(1, [0, 1, 2, 3])
@@ -513,7 +504,12 @@ def rank_program(g, core, T, topo):
         for e in range(4):
             mm(4 + e, "eq", "es", 128 * e, "lq", "ls", H * rd, H * rd + H)
         for e in range(4):
-            copy("S" if e % 2 else "V", A("vt", e, 4 * H, 4), bank(4 + e))
+            copy("S" if e == 3 else "V", A("vt", e, 4 * H, 4), bank(4 + e))
+        if last:
+            no_, nr = A("nmo", 0, C), at(nrow, 0, C)
+            emit("S", lambda e: e.activation(no_[0], nr[0], Act.Identity, bias=float(H)), [no_], [nr])
+            dma("Y", (T.nm[:, :], []), A("nmo", 0, C, pstep=16))
+        else: gather("S", ("pr", C * (rd + 1)), ("par", 0), nu)
         quant("mq", "ms", 0, H, A("vt", 0, 4 * H))
         for e in range(4):
             mm(4 + e, "wq", "wp", 128 * e, "mq", "ms", 0, H)
@@ -527,11 +523,14 @@ def rank_program(g, core, T, topo):
             break
         scores(0)
         dd, hu, prow = A("shf", w, w + 28), new("lu"), ("pr", C * (rd + 1))
+        kd, bs = new("lf"), new("lf")
+        base = at(bs)
+        ts(at(kd), dd, kb, Op.mult)
         copy("V", at(hu), A("shf", w + 28, w + 56))
+        tt(base, cl, at(kd), Op.subtract)
         signs(0, [0])
-        signs(1)
-        signs(0, [1, 2])
-        pending = [lambda prow=prow, nu=nu: gather("S", prow, ("par", 0), nu)]
+        signs(1, [0])
+        pending = [lambda: (signs(1, [1, 2]), signs(0, [1, 2]))]
 
     for s in sorted(total):
         if clock["G"].get(s, 0) < total[s]:

@@ -10,7 +10,7 @@ SCRATCH = {
     "xh": ("sbuf", [128, 4 * C], "bfloat16"),
     "xb": ("sbuf", [128, 4 * C], "bfloat16"),
     "tmp": ("sbuf", [128, 4 * C], "float32"),
-    "za": ("sbuf", [128, 2 * 4 * H], "bfloat16"),
+    "zn": ("sbuf", [128, 4 * C], "bfloat16"),
     "zt": ("sbuf", [128, 4 * H], "bfloat16"),
     "vt": ("sbuf", [128, 4 * C], "bfloat16"),
     "ut": ("sbuf", [128, 512], "bfloat16"),
@@ -239,9 +239,12 @@ def rank_program(g, core, T, topo):
     iota(A("ri", 0, 16), [[1, 16]], 128, -1)
     iota(A("ri", 32, 48), [[1, 16]], 0, 0)
     iota(A("iot", 0, C), [[1, C]], -H, 0, True)
-    iota(A("pk", 0, 8), [[16, 8]], 112, 0)
-    iota(A("pk", 16, 24), [[16, 8]], 1, 0)
-    iota(A("pk", 32, 40), [[16, 8]], 2, 0)
+    memset(A("one", 0, 512), 1.0)
+    memset(A("sg", 28, 32), 0.0)
+    iota(A("pk", 0, 1), [[1, 1]], 112, 0)
+    iota(A("pk", 1, 8), [[16, 7]], 0, 0)
+    iota(A("pk", 8, 16), [[16, 8]], 1, 0)
+    iota(A("pk", 16, 24), [[16, 8]], 2, 0)
     p15, p15f = A("pc", 1, 2), A("pf", 3, 4)
     r15, odd16 = A("ri", 64, 80), A("hs", 48, 64)
     ts(p15, A("pc", 0, 1), 15, Op.bitwise_and)
@@ -278,16 +281,13 @@ def rank_program(g, core, T, topo):
     gather("S", prow, ("par", 0), ("nu2", 0))
     gather("S", drs, ixs, ("nu2", 28))
     ts(cl, A("ci", 0, 28), p15f, Op.add)
-    ts(A("pk", 8, 16), A("pk", 0, 8), 127, Op.bitwise_and)
-    ts(kc1, kc, -1.0, Op.add)
+    copy("V", A("pu", 0, 24), A("pk", 0, 24))
     ts(ck, cl, kc, Op.add)
-    copy("V", A("pu", 0, 8), A("pk", 8, 16))
-    copy("V", A("pu", 16, 24), A("pk", 16, 24))
-    copy("V", A("pu", 32, 40), A("pk", 32, 40))
+    emit("S", lambda e: e.activation(kc1[0], kc[0], Act.Identity, bias=-1.0), [kc1], [kc])
     quant("uq", "us", 0, 128, A("ut", 0, 512))
 
     def side(k):
-        off = A("pu", 16 * k, 16 * k + 8)
+        off = A("pu", 8 * k, 8 * k + 8)
         o, w = A("pq", 128 * k, 128 * k + 128, bits=dt.uint32), ind(A("uq", 0, 128, bits=dt.uint32), off)
         copy("V", o, w)
         copy("S", A("ps", 128 * k, 128 * k + 128), ind(A("us", 0, 128), off))
@@ -326,7 +326,7 @@ def rank_program(g, core, T, topo):
         scores(k, [0])
     others(ix0, A("nxu2", 0, 28))
     gather("S", drow, ix0, ("nu2", 0))
-    for k in (1, 0): signs(k, [0])
+    for k in (1, 0): act(A("fl", half[k][0], half[k][1]), bank(banks[k][0]), Act.Sign)
     v = scan(drs)
     odd = new("lf")
     copy("V", at(odd), A("nb2", 28, 56))
@@ -341,10 +341,8 @@ def rank_program(g, core, T, topo):
         for k in (1, 0):
             scores(k, [1, 2])
             signs(k, [1])
-        memset(A("sg", 0, 128), 0.0)
 
     one = A("one", 0, 512)
-    memset(one, 1.0)
     for b in range(4):
         et = A("et", 512 * b, 512 * b + 512)
         emit("G", lambda e: e.affine_select(et[0], one[0], [[1, 512]], Op.is_equal, 0.0, -b, -4), [et], [one])
@@ -352,12 +350,12 @@ def rank_program(g, core, T, topo):
     def planes(k, es=(0, 1, 2, 3)):
         a, b = half[k]
         for e in es:
-            copy("S", A("xh", C * e + a, C * e + b), A("xt", 4 * a + e, 4 * b, 4), 0.5)
+            copy("S", A("xh", C * e + a, C * e + b), A("xt", 4 * a + e, 4 * b, 4))
 
-    def planes32(k):
+    def planes32(qn, k):
         a, b = half[k]
         for e in range(4):
-            copy("S", A("xb", C * e + a, C * e + b), A("xt", 4 * a + e, 4 * b, 4), 32.0)
+            copy(qn, A("xb", C * e + a, C * e + b), A("xt", 4 * a + e, 4 * b, 4), 32.0)
 
     def shift():
         i, o = A("sg", 0, 32), A("sg", 48, 80)
@@ -400,7 +398,9 @@ def rank_program(g, core, T, topo):
             for fn in late: fn()
             gather("S", n2, nrow, su)
             if j == 1: planes(1)
-            elif rd: planes(0, (0, 1))
+            elif rd:
+                signs(1, [2])
+                signs(0, [2])
             pv = scan(p2)
             v = scan(d2)
             odd = new("lf")
@@ -424,7 +424,9 @@ def rank_program(g, core, T, topo):
         offsets(scan(ix), iu)
         remote(q, A("linv", 32 * rd, 32 * rd + 28), at(iu), "ri%d" % rd, "ki%d" % rd)
         others_list = iu
-        planes(0, (0, 1, 2, 3) if rd == 0 else (2, 3))
+        planes(0)
+        for e in range(4):
+            tt(A("zn", C * e, C * e + C), ind(A("xh", C * e, C * e + C), at(iu)), A("xt", e, 4 * C, 4), Op.add)
         offsets(scan(nrow, H, C, no), nu, 14, 28)
         nv = at(no, 15, C, 16)
         n2i, n1, b2, nx, nxu = new("li"), new("li"), new("li"), new("li"), new("lu")
@@ -433,39 +435,30 @@ def rank_program(g, core, T, topo):
         ts(at(b2), at(n2i), 2, Op.bitwise_and)
         arrive([A("lreq", 32 * rd, 32 * rd + 14)], "rr%d" % rd, nq_)
         nq = ("lreq", 32 * rd)
-        for e in range(4):
-            gather("S", ("za", H * e), ("xh", C * e), nq, 0, H)
-        brow = new("rows")
-        gather("V", brow, ix, nq, 0, H)
-        bu = offsets(scan(brow, 0, H), None, 0, 14)
 
-        def means(out, step0, first_, lu, a):
+        def pick(qs, out, first_, lu, a):
             for e in range(4):
-                tt(A(out, step0 + e, step0 + 4 * H, 4), ind(A("xh", C * e, C * e + C), at(lu, a, a + 14)), A("za", first_ + H * e, first_ + H * e + H), Op.add)
-        means("zt", 0, 0, bu, 0)
+                copy(qs[e], A(out, first_ + e, first_ + 4 * H, 4), ind(A("zn", C * e, C * e + C), at(lu, a, a + 14)), 0.5)
+        pick("SSSS", "zt", 0, nq, 0)
         quant("zq", "zs", H * rd, H * rd + H, A("zt", 0, 4 * H))
         remote(q, A("lq", H * rd, H * rd + H, bits=dt.uint8), A("zq", H * rd, H * rd + H, bits=dt.uint8), "rc%d" % rd, "kc%d" % rd)
         remote(q, A("ls", H * rd, H * rd + H), A("zs", H * rd, H * rd + H), "rc%d" % rd, "kc%d" % rd)
         arrive([A("linv", 32 * rd, 32 * rd + 28)], "ri%d" % rd, np_)
-        drow, ip, mrow, er, dr = new("rows"), new("rows"), new("rows"), new("rows"), new("rows")
+        drow, ip, mrow, er = new("rows"), new("rows"), new("rows"), new("rows")
         gather("S", ip, IOT, ("linv", 32 * rd))
         tt(at(nx), at(n1), at(b2), Op.subtract)
         if not last:
             odd = new("lf")
             copy("V", at(odd), at(b2), 0.5)
         copy("V", at(nxu), at(nx))
-        gather("S", drow, ix, nu)
         both(mrow, ip, nxu, H, C)
         mu = offsets(scan(mrow, H, C), None, 14, 28)
+        if not last: gather("S", drow, ix, nu)
         gather("V", er, nrow, mu, H, C)
-        gather("S", dr, drow, mu, H, C)
         eu = offsets(scan(er, H, C), None, 14, 28)
-        du = offsets(scan(dr, H, C), None, 14, 28)
-        for e in range(4):
-            copy("S", A("za", 4 * H + H * e, 4 * H + H * e + H), ind(A("xh", C * e, C * e + C), at(eu, 14, 28)))
-        planes32(1)
-        planes32(0)
-        means("vt", 4 * H, 4 * H, du, 14)
+        pick("VSVS", "vt", 4 * H, eu, 14)
+        if not last: gather("S", ("pr", C * (rd + 1)), ("par", 0), nu)
+        planes32("S", 1)
         quant("mq", "ms", H, C, A("vt", 4 * H, 4 * C))
         for e in range(4):
             mm(e, "wq", "wp", 128 * e, "mq", "ms", H, C)
@@ -499,29 +492,29 @@ def rank_program(g, core, T, topo):
             copy("S" if k else "V", A("yo", a, b), bank(bk))
             dma("Y", (T.y[:, a:b], []), A("yo", a, b))
 
-        new_state(1, [0, 1, 2, 3])
         arrive([A("lq", H * rd, H * rd + H), A("ls", H * rd, H * rd + H)], "rc%d" % rd, 2 * np_)
         for e in range(4):
             mm(4 + e, "eq", "es", 128 * e, "lq", "ls", H * rd, H * rd + H)
         for e in range(4):
-            copy("S" if e == 3 else "V", A("vt", e, 4 * H, 4), bank(4 + e))
-        if last:
-            no_, nr = A("nmo", 0, C), at(nrow, 0, C)
-            emit("S", lambda e: e.activation(no_[0], nr[0], Act.Identity, bias=float(H)), [no_], [nr])
-            dma("Y", (T.nm[:, :], []), A("nmo", 0, C, pstep=16))
-        else: gather("S", ("pr", C * (rd + 1)), ("par", 0), nu)
+            copy("S", A("vt", e, 4 * H, 4), bank(4 + e))
+        new_state(1, [0, 1, 2, 3])
+        planes32("V", 0)
         quant("mq", "ms", 0, H, A("vt", 0, 4 * H))
         for e in range(4):
             mm(4 + e, "wq", "wp", 128 * e, "mq", "ms", 0, H)
-        states(1)
-        if last: finish(1)
-        else: scores(1)
         new_state(0, [4, 5, 6, 7])
+        states(1)
         states(0)
         if last:
+            no_, nr = A("nmo", 0, C), at(nrow, 0, C)
+            emit("S", lambda e: e.activation(no_[0], nr[0], Act.Identity, bias=float(H)), [no_], [nr])
+            finish(1)
             finish(0)
+            dma("Y", (T.nm[:, :], []), A("nmo", 0, C, pstep=16))
             break
-        scores(0)
+        for j in range(3):
+            scores(1, [j])
+            scores(0, [j])
         dd, hu, prow = A("shf", w, w + 28), new("lu"), ("pr", C * (rd + 1))
         kd, bs = new("lf"), new("lf")
         base = at(bs)
@@ -530,7 +523,7 @@ def rank_program(g, core, T, topo):
         tt(base, cl, at(kd), Op.subtract)
         signs(0, [0])
         signs(1, [0])
-        pending = [lambda: (signs(1, [1, 2]), signs(0, [1, 2]))]
+        pending = [lambda: (signs(1, [1]), signs(0, [1]))]
 
     for s in sorted(total):
         if clock["G"].get(s, 0) < total[s]:

from concourse.mybir import dt, AluOpType, ActivationFunctionType

C, H = 448, 224
STEP = [1, 2, 3]
K, BIG = 512.0, 2048.0
NROW, NLIST, NHALF, NSIGN = 32, 48, 16, 10

SCRATCH = {
    "xt": ("sbuf", [128, 4 * C], "bfloat16"),
    "xh": ("sbuf", [128, 4 * C], "bfloat16"),
    "xb": ("sbuf", [128, 4 * C], "bfloat16"),
    "tmp": ("sbuf", [128, 4 * C], "float32"),
    "zn": ("sbuf", [128, 4 * C], "bfloat16"),
    "zt": ("sbuf", [128, 4 * H], "bfloat16"),
    "vt": ("sbuf", [128, 4 * C], "bfloat16"),
    "ut": ("sbuf", [128, 512], "bfloat16"),
    "vi": ("sbuf", [128, 512], "bfloat16"),
    "one": ("sbuf", [128, 512], "bfloat16"),
    "et": ("sbuf", [128, 4 * 512], "bfloat16"),
    "yo": ("sbuf", [128, C], "float32"),
    "wq": ("sbuf", [128, 512], "float8_e4m3fn_x4"), "wp": ("sbuf", [128, 512], "uint8"),
    "uq": ("sbuf", [128, 128], "float8_e4m3fn_x4"), "us": ("sbuf", [128, 128], "uint8"),
    "pq": ("sbuf", [128, 384], "float8_e4m3fn_x4"), "ps": ("sbuf", [128, 384], "uint8"),
    "vq": ("sbuf", [128, 128], "float8_e4m3fn_x4"), "vs": ("sbuf", [128, 128], "uint8"),
    "eq": ("sbuf", [128, 512], "float8_e4m3fn_x4"), "es": ("sbuf", [128, 512], "uint8"),
    "xq": ("sbuf", [128, C], "float8_e4m3fn_x4"), "xs": ("sbuf", [128, C], "uint8"),
    "zq": ("sbuf", [128, 3 * H], "float8_e4m3fn_x4"), "zs": ("sbuf", [128, 3 * H], "uint8"),
    "lq": ("sbuf", [128, 3 * H], "float8_e4m3fn_x4"), "ls": ("sbuf", [128, 3 * H], "uint8"),
    "mq": ("sbuf", [128, C], "float8_e4m3fn_x4"), "ms": ("sbuf", [128, C], "uint8"),
    "rows": ("sbuf", [128, NROW * C], "bfloat16"), "nmo": ("sbuf", [128, C], "float32"), "hr": ("sbuf", [128, NHALF * C], "float16"), "fr": ("sbuf", [128, NSIGN * C], "bfloat16"),
    "lf": ("sbuf", [128, NLIST * 32], "float32"),
    "lu": ("sbuf", [128, NLIST * 32], "uint16"),
    "li": ("sbuf", [128, NLIST * 32], "int32"),
    "fl": ("sbuf", [128, 3 * C], "bfloat16"),
    "pr": ("sbuf", [128, 3 * C], "bfloat16"),
    "nl2": ("sbuf", [128, 56], "int32"), "nb2": ("sbuf", [128, 56], "int32"),
    "nw2": ("sbuf", [128, 56], "int32"), "nx2": ("sbuf", [128, 56], "int32"),
    "nu2": ("sbuf", [128, 56], "uint16"), "nxu2": ("sbuf", [128, 56], "uint16"),
    "own": ("sbuf", [128, 2 * 64], "float32"), "shf": ("sbuf", [128, 2 * 64], "float32"),
    "sg": ("sbuf", [128, 128], "float32"),
    "req": ("sbuf", [128, 3 * 32], "uint16"), "inv": ("sbuf", [128, 3 * 32], "uint16"),
    "lreq": ("sbuf", [128, 3 * 32], "uint16"), "linv": ("sbuf", [128, 3 * 32], "uint16"),
    "iot": ("sbuf", [128, C], "bfloat16"), "par": ("sbuf", [128, C], "bfloat16"),
    "hh": ("sbuf", [128, C], "float16"), "hb": ("sbuf", [128, C], "bfloat16"),
    "hs": ("sbuf", [128, 96], "float32"), "ri": ("sbuf", [128, 96], "int32"), "tu": ("sbuf", [128, 32], "uint16"),
    "pc": ("sbuf", [128, 8], "int32"), "pf": ("sbuf", [128, 8], "float32"),
    "ci": ("sbuf", [128, 32], "int32"), "cl": ("sbuf", [128, 64], "float32"),
    "pk": ("sbuf", [128, 48], "int32"), "pu": ("sbuf", [128, 48], "uint16"),
    "pb": ("psum", [128, 4096], "float32"),
}
SEMAPHORES = ["sv", "ss", "st", "sg"] + ["d%d" % k for k in range(64)] + ["%s%d" % (n, k) for n in ("rr", "ri", "rc", "kr", "ki", "kc") for k in range(3)]


def overlap(a, b):
    if a[0] != b[0] or a[2] <= b[1] or b[2] <= a[1] or a[4] <= b[3] or b[4] <= a[3]:
        return False
    if a[5] == b[5] and a[5] > 1:
        return (a[3] - b[3]) % a[5] == 0
    return True


def covers(a, b):
    if a[1] > b[1] or a[2] < b[2] or a[3] > b[3] or a[4] < b[4]:
        return False
    return a[5] == 1 or (a[5] == b[5] and (a[3] - b[3]) % a[5] == 0)


def rank_program(g, core, T, topo):
    rank = T.rank_of(core)
    if rank is None:
        return
    Op, Act = AluOpType, ActivationFunctionType
    queue = {"V": g.vector, "S": g.scalar, "P": g.tensor, "G": g, "Y": g.sync}
    esem = {"V": "sv", "S": "ss", "P": "st", "G": "sg"}
    total, clock, log, nd, count = {}, {q: {} for q in queue}, {}, [0], [0]

    def region(name, c0, c1, step=1, p0=0, p1=128):
        if name == "pb":
            return (name, 0, 128, c0 // 512 * 512, (c1 + 511) // 512 * 512, 1)
        return (name, p0, p1, c0, c1, step)

    def A(name, c0, c1, step=1, p0=0, p1=128, pstep=1, bits=None):
        t = T[name]
        rows = slice(None) if (p0, p1, pstep) == (0, 128, 1) else slice(p0, p1, pstep) if pstep > 1 else slice(p0, p1)
        ap = t[rows, c0:c1] if step == 1 else t[rows, c0:c1:step]
        if bits is not None: ap = ap.bitcast(bits)
        return (ap, [region(name, c0, c1, step, p0, p1)])

    def ind(win, off):
        return (win[0].indirect(off[0]), win[1] + off[1])

    def deps_of(q, ins, outs, dma):
        deps = []
        for reg in ins:
            for kind, r, op in log.get(reg[0], []):
                if overlap(reg, r):
                    if kind == "w": deps.append(op)
                    elif reg[0] == "pb" and op["q"] != q: deps.append(op)
        for reg in outs:
            for kind, r, op in log.get(reg[0], []):
                if overlap(reg, r):
                    if kind == "r" and op["q"] == q and not op["dma"] and not dma: continue
                    deps.append(op)
        return deps

    def waits(q, deps):
        ck = clock[q]
        for op in sorted(deps, key=lambda o: -o["n"]):
            if ck.get(op["sem"], 0) < op["val"]:
                queue[q].wait_ge(T.sem[op["sem"]], op["val"])
                for s, v in op["clock"].items(): ck[s] = max(ck.get(s, 0), v)
                ck[op["sem"]] = max(ck.get(op["sem"], 0), op["val"])

    def record(op, ins, outs):
        count[0] += 1
        op["n"] = count[0]
        for reg in outs:
            log[reg[0]] = [e for e in log.get(reg[0], []) if not covers(reg, e[1])] + [("w", reg, op)]
        for reg in ins:
            log.setdefault(reg[0], []).append(("r", reg, op))

    def emit(q, fn, outs, ins, dma=False):
        ri = [r for x in ins for r in x[1]]
        ro = [r for x in outs for r in x[1]]
        waits(q, deps_of(q, ri, ro, dma))
        inst = fn(queue[q])
        if dma:
            sem = "d%d" % nd[0]
            nd[0] += 1
            n = 16
        else:
            sem, n = esem[q], 1
        inst.then_inc(T.sem[sem], n)
        total[sem] = total.get(sem, 0) + n
        record({"q": q, "dma": dma, "sem": sem, "val": total[sem], "clock": dict(clock[q])}, ri, ro)

    def dma(q, out, in_):
        emit(q, lambda e: e.dma_start(out[0], in_[0]), [out], [in_], True)

    def src(name, c0=None, c1=None, p0=None, p1=None):
        return (T[name][slice(p0, p1), slice(c0, c1)], [])

    def copy(q, out, in_, scale=None):
        if q == "V":
            if scale is None: emit("V", lambda e: e.tensor_copy(out[0], in_[0]), [out], [in_])
            else: emit("V", lambda e: e.tensor_scalar(out[0], in_[0], scale, None, Op.mult), [out], [in_])
        elif scale is None: emit("S", lambda e: e.activation(out[0], in_[0], Act.Copy), [out], [in_])
        else: emit("S", lambda e: e.activation(out[0], in_[0], Act.Copy, scale=scale), [out], [in_])

    def act(out, in_, func):
        emit("S", lambda e: e.activation(out[0], in_[0], func), [out], [in_])

    def tt(out, a, b, op):
        emit("V", lambda e: e.tensor_tensor(out[0], a[0], b[0], op), [out], [a, b])

    def ts(out, a, s1, op0, s2=None, op1=None):
        ins = [a] + [s for s in (s1, s2) if isinstance(s, tuple)]
        v1 = s1[0] if isinstance(s1, tuple) else s1
        v2 = s2[0] if isinstance(s2, tuple) else s2
        if op1 is None: emit("V", lambda e: e.tensor_scalar(out[0], a[0], v1, None, op0), [out], ins)
        else: emit("V", lambda e: e.tensor_scalar(out[0], a[0], v1, v2, op0, op1), [out], ins)

    def quant(qn, sn, a, b, tile):
        o, s = A(qn, a, b), A(sn, a, b)
        emit("V", lambda e: e.quantize_mx(o[0], s[0], tile[0]), [o, s], [tile])

    def mm(bank, sq, sp, a, mq, mp, b0, b1):
        out, l, ls, r, rs = A("pb", 512 * bank, 512 * bank + b1 - b0), A(sq, a, a + 128), A(sp, a, a + 128), A(mq, b0, b1), A(mp, b0, b1)
        emit("P", lambda e: e.matmul_mx(out[0], l[0], ls[0], r[0], rs[0], True, True), [out], [l, ls, r, rs])

    def bank(k, n=H):
        return A("pb", 512 * k, 512 * k + n)

    pool = {"rows": [0], "lf": [0], "lu": [0], "li": [0], "fr": [0], "hr": [0]}
    size = {"rows": NROW, "lf": NLIST, "lu": NLIST, "li": NLIST, "fr": NSIGN, "hr": NHALF}

    def new(kind):
        k = pool[kind][0] % size[kind]
        pool[kind][0] += 1
        return (kind, k * (C if kind in ("rows", "fr", "hr") else 32))

    def at(slot, a=0, b=28, step=1):
        return A(slot[0], slot[1] + a, slot[1] + b, step)

    IOT = ("iot", 0)
    kc, kb, kc1 = A("pf", 0, 1), A("pf", 1, 2), A("pf", 2, 3)
    cl, ck = A("cl", 0, 28), A("cl", 32, 60)

    def gather(q, out, win, lu, a=0, b=C):
        copy(q, at(out, a, b), ind(at(win, 0, C), at(lu, a // 16, b // 16)))

    def both(out, win, lu, a=0, b=C):
        h = (b - a) // 64 * 32
        gather("S", out, win, lu, a + h, b)
        gather("V", out, win, lu, a, a + h)

    def scan(row, a=0, b=C, o=None):
        o = o or new("hr" if row[0] == "rows" else "fr")
        hold, r, out = A("hh" if row[0] == "rows" else "hb", 0, b - a), at(row, a, b), at(o, a, b)
        emit("V", lambda e: e.tensor_tensor_scan(out[0], hold[0], r[0], 0.0, Op.add, Op.max), [out], [hold, r])
        return at(o, a + 15, b, 16)

    def offsets(v, out=None, a=0, b=28):
        out = out or new("lu")
        ts(at(out, a, b), v, kc, Op.subtract)
        return out

    def remote(dst, out, in_, rsem, lsem):
        rid, pid, _ = topo.addr(dst)
        waits("G", deps_of("G", in_[1], [], True))
        n = len(topo.engines(core, dst))
        g.remote_dma(out[0], in_[0], T.sem[rsem], T.sem[lsem], pid, rid, topo.mask(core, dst))
        total[lsem] = total.get(lsem, 0) + n
        record({"q": "G", "dma": True, "sem": lsem, "val": total[lsem], "clock": dict(clock["G"])}, in_[1], [])

    def arrive(outs, sem, n):
        total[sem] = n
        record({"q": "R", "dma": True, "sem": sem, "val": n, "clock": {}}, [], [r for o in outs for r in o[1]])

    dma("Y", A("nl2", 28, 56, p0=16), src("nl", p0=0, p1=112))
    dma("S", A("nl2", 28, 56, p0=0, p1=16), src("nl", p0=112, p1=128))
    dma("Y", A("nl2", 0, 28), src("nl"))
    dma("S", A("ut", 0, 512), src("u"))
    dma("Y", A("xt", 4 * H, 4 * C), src("x", 4 * H, 4 * C))
    dma("S", A("xt", 0, 4 * H), src("x", 0, 4 * H))
    dma("Y", A("wq", 0, 512, bits=dt.uint8), src("wc"))
    dma("Y", A("wp", 0, 512), src("ws"))
    dma("Y", A("vi", 0, 512), src("v"))

    def iota(out, pattern, base, cm, f=False):
        if f: emit("G", lambda e: e.iota(out[0], pattern, base, cm, allow_small_or_imprecise_dtypes=True), [out], [])
        else: emit("G", lambda e: e.iota(out[0], pattern, base, cm), [out], [])

    def memset(out, k):
        emit("V", lambda e: e.memset(out[0], k), [out], [])

    iota(A("pc", 0, 1), [[1, 1]], 0, 1)
    iota(A("ci", 0, 28), [[16, 28]], 0, 0)
    iota(A("ri", 0, 16), [[1, 16]], 128, -1)
    iota(A("ri", 32, 48), [[1, 16]], 0, 0)
    iota(A("iot", 0, C), [[1, C]], -H, 0, True)
    memset(A("one", 0, 512), 1.0)
    memset(A("sg", 28, 32), 0.0)
    iota(A("pk", 0, 1), [[1, 1]], 112, 0)
    iota(A("pk", 1, 8), [[16, 7]], 0, 0)
    iota(A("pk", 8, 16), [[16, 8]], 1, 0)
    iota(A("pk", 16, 24), [[16, 8]], 2, 0)
    p15, p15f = A("pc", 1, 2), A("pf", 3, 4)
    r15, odd16 = A("ri", 64, 80), A("hs", 48, 64)
    ts(p15, A("pc", 0, 1), 15, Op.bitwise_and)
    ts(r15, A("ri", 0, 16), 15, Op.bitwise_and)
    ts(A("ri", 48, 64), A("ri", 32, 48), 1, Op.bitwise_and)
    copy("V", p15f, p15)
    ts(A("hs", 0, 16), r15, 0.0, Op.is_equal, -BIG, Op.mult)
    ts(A("hs", 16, 32), r15, 1.0, Op.is_equal, K, Op.mult)
    copy("V", odd16, A("ri", 48, 64))
    ts(A("tu", 0, 28), A("ci", 0, 28), 0.0, Op.mult, p15f, Op.add)
    tt(A("hs", 32, 48), A("hs", 0, 16), A("hs", 16, 32), Op.add)
    ts(A("pf", 4, 5), p15, 15.0, Op.is_lt, K, Op.mult)
    ts(kb, p15, 15.0, Op.is_lt, 2.0, Op.mult)
    ts(kc, A("pf", 4, 5), -float(H), Op.add)
    hold16 = A("hs", 32, 48)
    copy("S", A("hh", 0, C), ind(hold16, A("tu", 0, 28)))
    copy("S", A("hb", 0, C), ind(hold16, A("tu", 0, 28)), 1.0 / 256)
    copy("S", A("par", 0, C), ind(odd16, A("tu", 0, 28)))

    ts(A("nb2", 0, 56), A("nl2", 0, 56), 1, Op.bitwise_and)
    copy("V", A("nu2", 0, 56), A("nl2", 0, 56))
    ts(A("nw2", 0, 56), A("nb2", 0, 56), -2.0, Op.mult, 1.0, Op.add)
    tt(A("nx2", 0, 56), A("nl2", 0, 56), A("nw2", 0, 56), Op.add)
    copy("V", A("nxu2", 0, 56), A("nx2", 0, 56))

    def others(out, nx):
        o, i = at(out, 0, C), A("iot", 0, C)
        w = ind(o, nx)
        emit("V", lambda e: e.tensor_copy(w[0], i[0]), [o], [i, nx])

    ixs, ix0, drs, drow, nrow, prow = new("rows"), new("rows"), new("rows"), new("rows"), new("rows"), ("pr", 0)
    others(ixs, A("nxu2", 28, 56))
    gather("S", nrow, IOT, ("nu2", 0))
    gather("S", prow, ("par", 0), ("nu2", 0))
    gather("S", drs, ixs, ("nu2", 28))
    ts(cl, A("ci", 0, 28), p15f, Op.add)
    copy("V", A("pu", 0, 24), A("pk", 0, 24))
    ts(ck, cl, kc, Op.add)
    emit("S", lambda e: e.activation(kc1[0], kc[0], Act.Identity, bias=-1.0), [kc1], [kc])
    quant("uq", "us", 0, 128, A("ut", 0, 512))

    def side(k):
        off = A("pu", 8 * k, 8 * k + 8)
        o, w = A("pq", 128 * k, 128 * k + 128, bits=dt.uint32), ind(A("uq", 0, 128, bits=dt.uint32), off)
        copy("V", o, w)
        copy("S", A("ps", 128 * k, 128 * k + 128), ind(A("us", 0, 128), off))

    half = [(0, H), (H, C)]

    def states(k):
        a, b = half[k]
        quant("xq", "xs", a, b, A("xt", 4 * a, 4 * b))

    banks = [[3, 4, 5], [0, 1, 2]]

    def scores(k, js=(0, 1, 2)):
        for j in js:
            mm(banks[k][j], "pq", "ps", 128 * j, "xq", "xs", half[k][0], half[k][1])

    def signs(k, js=(0, 1, 2)):
        for j in js:
            o, i = A("fl", C * j + half[k][0], C * j + half[k][1]), bank(banks[k][j])
            if j == 0 and k == 0: ts(o, i, 0.0, Op.is_gt)
            else: act(o, i, Act.Sign)

    def pairs(v, odd):
        t, kd, h, dd, base, hu = new("lf"), new("lf"), new("lf"), new("lf"), new("lf"), new("lu")
        tt(at(dd), v, ck, Op.subtract)
        tt(at(t), at(odd), at(dd), Op.mult)
        ts(at(kd), at(dd), kb, Op.mult)
        tt(at(h), at(t), cl, Op.add)
        tt(at(base), cl, at(kd), Op.subtract)
        copy("V", at(hu), at(h))
        return at(dd), at(base), hu

    side(0)
    for k in (1, 0):
        states(k)
        scores(k, [0])
    others(ix0, A("nxu2", 0, 28))
    gather("S", drow, ix0, ("nu2", 0))
    for k in (1, 0): act(A("fl", half[k][0], half[k][1]), bank(banks[k][0]), Act.Sign)
    v = scan(drs)
    odd = new("lf")
    copy("V", at(odd), A("nb2", 28, 56))
    dd, base, hu = pairs(v, odd)

    def second():
        side(1)
        side(2)
        return offsets(scan(ix0))

    def third():
        for k in (1, 0):
            scores(k, [1, 2])
            signs(k, [1])

    one = A("one", 0, 512)
    for b in range(4):
        et = A("et", 512 * b, 512 * b + 512)
        emit("G", lambda e: e.affine_select(et[0], one[0], [[1, 512]], Op.is_equal, 0.0, -b, -4), [et], [one])

    def planes(k, es=(0, 1, 2, 3)):
        a, b = half[k]
        for e in es:
            copy("S", A("xh", C * e + a, C * e + b), A("xt", 4 * a + e, 4 * b, 4))

    def planes32(qn, k):
        a, b = half[k]
        for e in range(4):
            copy(qn, A("xb", C * e + a, C * e + b), A("xt", 4 * a + e, 4 * b, 4), 32.0)

    def shift():
        i, o = A("sg", 0, 32), A("sg", 48, 80)
        emit("V", lambda e: e.transpose(o[0], i[0]), [o], [i])
        for a in range(4):
            d = 32 * ((a + 1) % 4)
            copy("S" if a in (1, 2) else "V", A("sg", 32, 48, p0=d, p1=d + 32), A("sg", 64, 80, p0=32 * a, p1=32 * a + 32))
        i2, o2 = A("sg", 32, 64), A("sg", 96, 128)
        emit("V", lambda e: e.transpose(o2[0], i2[0]), [o2], [i2])
        return A("sg", 96, 124)

    pending, others_list = [], None
    for rd, step in enumerate(STEP):
        last = rd == 2
        p, q = T.cores[(rank - step) % 4], T.cores[(rank + step) % 4]
        np_, nq_ = len(topo.engines(core, p)), len(topo.engines(core, q))
        later, late = pending, []
        for j in range(3):
            frow = new("fr")
            act(at(frow, H, C), ind(A("fl", C * j, C * j + C), at(hu, 14, 28)), Act.Relu)
            ts(at(frow, 0, H), ind(A("fl", C * j, C * j + C), at(hu, 0, 14)), 0.0, Op.max)
            for fn in later: fn()
            v = scan(frow)
            t, s, su = new("lf"), new("lf") if j == 0 else ("sg", 0), new("lu")
            tt(at(t), v, dd, Op.mult)
            tt(at(s), at(t), base, Op.add)
            if j: copy("V", at(su), shift())
            else: copy("V", at(su), at(s))
            n2, srow = new("rows"), new("rows")
            if j == 2: break
            e1, p2, d2, xr = new("rows"), new("fr"), new("rows"), new("rows")
            both(e1, drow, su)
            gather("S", srow, IOT, su)
            eu = offsets(scan(e1))
            gather("V", p2, prow, su)
            gather("S", d2, srow, eu)
            if rd == 0 and j == 0:
                others_list = second()
                third()
            for fn in late: fn()
            gather("S", n2, nrow, su)
            if j == 1: planes(1)
            elif rd:
                signs(1, [2])
                signs(0, [2])
            pv = scan(p2)
            v = scan(d2)
            odd = new("lf")
            ts(at(odd), pv, kb, Op.subtract)
            dd, base, hu = pairs(v, odd)
            drow, nrow, prow, xl, others_list = d2, n2, p2, others_list, new("lu")
            later = [lambda xr=xr, srow=srow, xl=xl: gather("S", xr, srow, xl)]
            late = [lambda xr=xr, lu=others_list: offsets(scan(xr), lu)]
            if rd == 0 and j == 0: later.append(lambda: [signs(k, [2]) for k in (1, 0)])
        no, nu = new("hr"), ("req", 32 * rd)
        gather("S", srow, IOT, su)
        gather("V", n2, nrow, su, 0, H)
        offsets(scan(n2, 0, H, no), nu, 0, 14)
        remote(p, A("lreq", 32 * rd, 32 * rd + 14), at(nu, 0, 14), "rr%d" % rd, "kr%d" % rd)
        for fn in late: fn()
        ix = new("rows")
        gather("S", n2, nrow, su, H, C)
        nrow = n2
        both(ix, srow, others_list)
        iu = ("inv", 32 * rd)
        offsets(scan(ix), iu)
        remote(q, A("linv", 32 * rd, 32 * rd + 28), at(iu), "ri%d" % rd, "ki%d" % rd)
        others_list = iu
        planes(0)
        for e in range(4):
            tt(A("zn", C * e, C * e + C), ind(A("xh", C * e, C * e + C), at(iu)), A("xt", e, 4 * C, 4), Op.add)
        offsets(scan(nrow, H, C, no), nu, 14, 28)
        nv = at(no, 15, C, 16)
        n2i, n1, b2, nx, nxu = new("li"), new("li"), new("li"), new("li"), new("lu")
        ts(at(n2i), nv, kc, Op.subtract, 2.0, Op.mult)
        ts(at(n1), nv, kc1, Op.subtract)
        ts(at(b2), at(n2i), 2, Op.bitwise_and)
        arrive([A("lreq", 32 * rd, 32 * rd + 14)], "rr%d" % rd, nq_)
        nq = ("lreq", 32 * rd)

        def pick(qs, out, first_, lu, a):
            for e in range(4):
                copy(qs[e], A(out, first_ + e, first_ + 4 * H, 4), ind(A("zn", C * e, C * e + C), at(lu, a, a + 14)), 0.5)
        pick("SSSS", "zt", 0, nq, 0)
        quant("zq", "zs", H * rd, H * rd + H, A("zt", 0, 4 * H))
        remote(q, A("lq", H * rd, H * rd + H, bits=dt.uint8), A("zq", H * rd, H * rd + H, bits=dt.uint8), "rc%d" % rd, "kc%d" % rd)
        remote(q, A("ls", H * rd, H * rd + H), A("zs", H * rd, H * rd + H), "rc%d" % rd, "kc%d" % rd)
        arrive([A("linv", 32 * rd, 32 * rd + 28)], "ri%d" % rd, np_)
        drow, ip, mrow, er = new("rows"), new("rows"), new("rows"), new("rows")
        gather("S", ip, IOT, ("linv", 32 * rd))
        tt(at(nx), at(n1), at(b2), Op.subtract)
        if not last:
            odd = new("lf")
            copy("V", at(odd), at(b2), 0.5)
        copy("V", at(nxu), at(nx))
        both(mrow, ip, nxu, H, C)
        mu = offsets(scan(mrow, H, C), None, 14, 28)
        if not last: gather("S", drow, ix, nu)
        gather("V", er, nrow, mu, H, C)
        eu = offsets(scan(er, H, C), None, 14, 28)
        pick("VSVS", "vt", 4 * H, eu, 14)
        if not last: gather("S", ("pr", C * (rd + 1)), ("par", 0), nu)
        planes32("S", 1)
        quant("mq", "ms", H, C, A("vt", 4 * H, 4 * C))
        for e in range(4):
            mm(e, "wq", "wp", 128 * e, "mq", "ms", H, C)
        if not last:
            t, w = new("lf"), 64 * rd
            v = scan(drow)
            tt(A("own", w, w + 28), v, ck, Op.subtract)
            tt(at(t), at(odd), A("own", w, w + 28), Op.mult)
            tt(A("own", w + 28, w + 56), at(t), cl, Op.add)
            dma("Y", A("shf", w, w + 56, p0=16), A("own", w, w + 56, p0=0, p1=112))
            dma("Y", A("shf", w, w + 56, p0=0, p1=16), A("own", w, w + 56, p0=112, p1=128))
        if rd == 0:
            for b in range(4):
                quant("eq", "es", 128 * b, 128 * b + 128, A("et", 512 * b, 512 * b + 512))
            quant("vq", "vs", 0, 128, A("vi", 0, 512))

        def new_state(k, banks):
            a, b = half[k]
            for e in range(4):
                o = A("tmp", C * e + a, C * e + b)
                tt(o, bank(banks[e]), A("xb", C * e + a, C * e + b), Op.add)
                copy("S", A("xt", 4 * a + e, 4 * b, 4), o, 0.03125)

        def finish(k):
            a, b = half[k]
            bk = 7 if k == 0 else 0
            mm(bk, "vq", "vs", 0, "xq", "xs", a, b)
            dma("Y", (T.oc[:, 4 * a:4 * b], []), A("xq", a, b, bits=dt.uint8))
            for i in range(4):
                dma("Y" if i % 2 else "S", (T.osc[4 * i:4 * i + 4, a:b], []), A("xs", a, b, p0=32 * i, p1=32 * i + 4))
            copy("S" if k else "V", A("yo", a, b), bank(bk))
            dma("Y", (T.y[:, a:b], []), A("yo", a, b))

        arrive([A("lq", H * rd, H * rd + H), A("ls", H * rd, H * rd + H)], "rc%d" % rd, 2 * np_)
        for e in range(4):
            mm(4 + e, "eq", "es", 128 * e, "lq", "ls", H * rd, H * rd + H)
        for e in range(4):
            copy("S", A("vt", e, 4 * H, 4), bank(4 + e))
        new_state(1, [0, 1, 2, 3])
        planes32("V", 0)
        quant("mq", "ms", 0, H, A("vt", 0, 4 * H))
        for e in range(4):
            mm(4 + e, "wq", "wp", 128 * e, "mq", "ms", 0, H)
        new_state(0, [4, 5, 6, 7])
        states(1)
        states(0)
        if last:
            no_, nr = A("nmo", 0, C), at(nrow, 0, C)
            emit("S", lambda e: e.activation(no_[0], nr[0], Act.Identity, bias=float(H)), [no_], [nr])
            finish(1)
            finish(0)
            dma("Y", (T.nm[:, :], []), A("nmo", 0, C, pstep=16))
            break
        for j in range(3):
            scores(1, [j])
            scores(0, [j])
        dd, hu, prow = A("shf", w, w + 28), new("lu"), ("pr", C * (rd + 1))
        kd, bs = new("lf"), new("lf")
        base = at(bs)
        ts(at(kd), dd, kb, Op.mult)
        copy("V", at(hu), A("shf", w + 28, w + 56))
        tt(base, cl, at(kd), Op.subtract)
        signs(0, [0])
        signs(1, [0])
        pending = [lambda: (signs(1, [1]), signs(0, [1]))]

    for s in sorted(total):
        if clock["G"].get(s, 0) < total[s]:
            g.wait_ge(T.sem[s], total[s])
